import numpy as np, ml_dtypes
CORES = [9,25,41,57]
N = 4
import mx_ref
BF = ml_dtypes.bfloat16
def pick(q, e):
    c = np.concatenate([q[0].reshape(128, -1, 4), np.zeros((128, 1, 4), np.uint8)], axis=1); s = np.concatenate([q[1], np.ones((16, 1), np.uint8)], axis=1)
    return (np.ascontiguousarray(c[:, e].reshape(128, -1)), np.ascontiguousarray(s[:, e]))
def join(*qs):
    return (np.concatenate([q[0] for q in qs], axis=1), np.concatenate([q[1] for q in qs], axis=1))
def put(q, e, v):
    c, s = q[0].reshape(128, -1, 4).copy(), q[1].copy(); c[:, e] = v[0].reshape(128, -1, 4); s[:, e] = v[1]
    return (c.reshape(128, -1), s)
def pk(c, s):
    return (np.ascontiguousarray(c), mx_ref.live(s))
def emit(q):
    return q[0], q[1]
def decode(q):
    o = []
    for b in range(4):
        e = np.zeros((128, 128, 4), np.float32); e[np.arange(128), np.arange(128), b] = 1
        o.append(mx_ref.matmul(mx_ref.quantize(e.reshape(128, 512).astype(BF)), q))
    return np.stack(o, axis=2).reshape(128, -1)
def f(rng, *shape):
    return mx_ref.flush((rng.standard_normal(shape, dtype=np.float32) * np.exp2(rng.integers(-2, 3, shape[:-1] + (1,)))).astype(BF))
def wide(rng, *shape, cols=0):
    v = rng.standard_normal(shape, dtype=np.float32) * np.exp2(rng.integers(-12, 13, shape)).astype(np.float32)
    if cols: v *= np.repeat(np.exp2(rng.integers(-cols, cols + 1, shape[:-2] + (1, shape[-1] // 4))) * (rng.random(shape[:-2] + (1, shape[-1] // 4)) > 0.0625), 4, axis=-1).astype(np.float32)
    return mx_ref.flush(v.astype(BF))
P, B, K, KO = 384, 96, 32, 32
def big(v):
    v = v.astype(np.float32)
    v[np.abs(v) < np.float32(2.0 ** -16)] = 0
    return v.astype(BF)
def toward(rng, u, size):
    sg = np.where(u[0, :, :4].astype(np.float32) < 0, -1.0, 1.0)
    s = np.asarray(size)[..., None, :, None]
    v = (1 + rng.random(s.shape[:-3] + (128, s.shape[-2], 4))) * sg[:, None, :] * s
    return v.reshape(v.shape[:-2] + (-1,)).astype(np.float32)
def near(rng, size):
    s = np.abs(np.asarray(size))[..., None, :, None]
    v = (rng.random(s.shape[:-3] + (128, s.shape[-2], 4)) - 0.5) * 0.25 * s
    return v.reshape(v.shape[:-2] + (-1,)).astype(np.float32)
def plain(rng):
    u = np.array(f(rng, 128, 512))
    u[:, 4:] = 0
    return {"gr": big(f(rng, N, 128, 4 * P)), "er": big(f(rng, N, 128, 4 * P).astype(np.float32) * np.float32(0.125)), "fo": big(f(rng, N, 128, 4 * B)), "u": np.stack([u] * N), "w": f(rng, N, 128, 512)}
def setup_inputs(rng):
    return plain(rng)
def setup_inputs_same(rng):
    d = plain(rng)
    size, own = np.full((B, N), 2.0 ** -5), np.full((N, B), 2.0 ** -4)
    for o in range(N):
        m = rng.permutation(B)
        size[m[:K], o] = np.exp2(rng.integers(0, 3, K))
        own[o, m[K:K + KO // 2]] = 2.0 ** 8
    size = size * rng.choice([-1.0, 1.0], size.shape)
    size = np.tile(size.reshape(P), (N, 1))
    own = own * rng.choice([-1.0, 1.0], own.shape)
    return {**d, "gr": big(toward(rng, d["u"], size)), "er": big(near(rng, size)), "fo": big(toward(rng, d["u"], own))}
def setup_inputs_apart(rng):
    d = plain(rng)
    size = np.full((N, B, N), 2.0 ** -5)
    for o in range(N):
        m, a = rng.permutation(B), rng.permutation(N)
        for s in range(N): size[s, m[(a[s] * K + np.arange(K)) % B], o] = np.exp2(rng.integers(0, 3, K))
    size = (size * rng.choice([-1.0, 1.0], size.shape)).reshape(N, P)
    e, fo = big(near(rng, size)), np.array(d["fo"])
    a = rng.permutation(N)
    e[a[0]] = 0
    fo[a[1]] = 0
    return {**d, "gr": big(toward(rng, d["u"], size)), "er": e, "fo": fo}
def setup_inputs_cancel(rng):
    d = plain(rng)
    size, own = np.full((B, N), 2.0 ** 5), np.full((N, B), 2.0 ** -13)
    gone = np.zeros(N, int)
    for o in range(N):
        m = rng.permutation(B)[:K]
        size[m, o] = np.exp2(rng.integers(11, 13, K))
        own[o, m] = np.exp2(rng.integers(-10, -8, K))
        own[o, m[:K // 2]] = 0
        gone[o] = m[K - 1]
    h = int(rng.integers(0, N))
    own[h] = 0
    size = np.tile(size.reshape(P), (N, 1)) * rng.choice([-1.0, 1.0], (N, P))
    g, e, fo = big(toward(rng, d["u"], size)), big(near(rng, size)), big(toward(rng, d["u"], own))
    a = rng.permutation(N)
    g[a[1::2]] = -g[a[::2]]
    e[a[1::2]] = -e[a[::2]]
    gv, ev, fv = g.reshape(N, 128, B, N, 4), e.reshape(N, 128, B, N, 4), fo.reshape(N, 128, B, 4)
    half = np.where(d["u"][0, :, :4].astype(np.float32) < 0, -1.0, 1.0) * 2.0 ** 11
    part = np.ones(N)
    part[a[1::2]] = -1
    part[a[:2]] = -1
    for o in range(N):
        if o == h: continue
        m, x = int(gone[o]), half * rng.choice([-1.0, 1.0])
        gv[:, :, m, o] = (part[:, None, None] * x).astype(BF)
        ev[:, :, m, o] = 0
        fv[o, :, m] = (2 * x).astype(BF)
    return {**d, "gr": g, "er": e, "fo": fo}
def setup_inputs_ties(rng):
    d = plain(rng)
    u = np.zeros((128, 512), BF)
    u[:, :4] = ((1 + rng.random((128, 4))) * 2.0 ** 29 * rng.choice([-1.0, 1.0], (128, 4))).astype(BF)
    d["u"] = np.stack([u] * N)
    size, own, tied = np.zeros((B, N)), np.ones((N, B)), np.zeros((N, B), bool)
    for o in range(N):
        t = int(rng.integers(2, min(K, KO)))
        m = rng.permutation(B)
        size[m[:t], o] = 2.0 ** 23
        size[int(m[:t].min()), o] = 7 * 2.0 ** 20
        own[o, m[:t]] = 2.0 ** 23
        tied[o, np.sort(m[t:])[K - t:]] = True
    size = np.tile(size.reshape(P), (N, 1))
    hot = np.repeat(size > 0, 4, axis=1)[:, None, :]
    sg = np.repeat(rng.choice([-1.0, 1.0], (N, P)), 4, axis=1)[:, None, :]
    g = np.where(hot, toward(rng, d["u"], size), np.tile(toward(rng, d["u"], np.ones((N, 1))), (1, 1, P)) * sg)
    e = np.where(hot, near(rng, size), np.tile(near(rng, np.ones((N, 1))), (1, 1, P)) * sg)
    so = np.repeat(rng.choice([-1.0, 1.0], (N, B)), 4, axis=1)[:, None, :]
    fo = np.where(np.repeat(tied, 4, axis=1)[:, None, :], np.tile(toward(rng, d["u"], np.full((N, 1), 2.0 ** 9)), (1, 1, B)) * so, toward(rng, d["u"], own))
    return {**d, "gr": big(g), "er": big(e), "fo": big(fo)}
def setup_inputs_spread(rng):
    g, e, fo = big(wide(rng, N, 128, 4 * P, cols=8)), big(wide(rng, N, 128, 4 * P, cols=8)), big(wide(rng, N, 128, 4 * B, cols=8))
    gv, ev, fv = g.reshape(N, 128, B, N, 4), e.reshape(N, 128, B, N, 4), fo.reshape(N, 128, B, 4)
    top = np.array([225.0, 241.0, 255.0])[np.arange(128) // 8 % 3][:, None]
    r = int(rng.integers(0, N))
    for o in range(N):
        z = np.sort(rng.permutation(B)[int(rng.integers(0, K)):])
        for v in (gv, ev):
            v[r][:, z, o] = 0
            v[:, :, int(z[0]), o] = 0
        fv[o, :, int(z[0])] = (top * np.exp2(rng.integers(-14, -10, (128, 4))) * rng.choice([-1.0, 1.0], (128, 4))).astype(BF)
    return {**plain(rng), "gr": g, "er": e, "fo": fo}
def check_inputs(d):
    b = []
    for k, lo, hi in (("gr", -16, 24), ("er", -16, 24), ("fo", -16, 24), ("u", -30, 30), ("w", -30, 30)):
        v = np.abs(d[k].astype(np.float32))
        if not (np.isfinite(v).all() and ((v == 0) | (v >= 2.0 ** lo) & (v <= 2.0 ** hi)).all()): b.append("a value of " + k)
    u = d["u"].astype(np.float32)
    if (u[:, :, 4:] != 0).any(): b.append("u has numbers behind its column 0")
    if (u != u[:1]).any(): b.append("u isn't the same on all ranks")
    return b
def best(z, k):
    return np.argsort(-np.abs(z), kind="stable")[:k]
def reference(gr, er, fo, u, w):
    oc, osc = np.zeros((N, 128, 4 * (P + B)), np.uint8), np.zeros((N, 16, P + B), np.uint8)
    nb, y = np.zeros((N, 1, N * KO), np.float32), np.zeros((N, 128, N * KO), np.float32)
    qu = [mx_ref.quantize(u[r]) for r in range(N)]
    sent, held, werr = [], [], []
    for s in range(N):
        v = (gr[s].astype(np.float32) + decode(mx_ref.quantize(er[s]))).astype(BF)
        q = mx_ref.quantize(v)
        z = mx_ref.matmul(qu[s], q)[0]
        e = [best(z[o::N], K) for o in range(N)]
        n = np.concatenate([N * e[o] + o for o in range(N)])
        dq = decode(q)
        left = mx_ref.quantize((v.astype(np.float32) - dq).astype(BF))
        werr.append(put(q, n, pick(left, n)))
        sent.append(e)
        held.append(dq.reshape(128, P, 4))
    win, numbers = [], []
    for o in range(N):
        qf = mx_ref.quantize(fo[o])
        a, named = decode(qf).reshape(128, B, 4).copy(), np.zeros(B, bool)
        for s in range(N):
            m = sent[s][o]
            a[:, m] = a[:, m] + held[s][:, N * m + o]
            named[m] = True
        a = a.reshape(128, 4 * B).astype(BF)
        m = np.flatnonzero(named)
        p = put(qf, m, pick(mx_ref.quantize(a), m))
        t = best(mx_ref.matmul(qu[o], p)[0], KO)
        left = mx_ref.quantize((a.astype(np.float32) - decode(p)).astype(BF))
        oc[o], osc[o] = emit(join(werr[o], put(p, t, pick(left, t))))
        win.append(pick(p, t))
        numbers.append(N * t + o)
    every = join(*win)
    for r in range(N):
        nb[r, 0] = np.concatenate(numbers)
        y[r] = mx_ref.matmul(mx_ref.quantize(w[r]), every)
    return {"oc": oc, "osc": osc, "nb": nb, "y": y}

@@ -1,0 +1,469 @@
+from concourse.bass import DstId, RemoteDMATransfer
+from concourse.mybir import dt, AluOpType, ActivationFunctionType
+
+N, P, B, K = 4, 384, 96, 32
+F32, BF, I32, U16, CODE, PLANE = "float32", "bfloat16", "int32", "uint16", "float8_e4m3fn_x4", "uint8"
+
+SCRATCH = {"ps": ("psum", [128, 4096], F32)}
+for _n, _w, _d in (
+        ("ert", 1536, BF), ("grt", 1536, BF), ("fot", 512, BF), ("wt", 512, BF), ("uc", 4, BF), ("ucf", 4, F32),
+        ("one", 512, BF), ("zt", 608, BF), ("ew", 520, BF), ("urep", 512, BF), ("tri", 96, BF), ("s16", 128, BF),
+        ("hh", 128, BF), ("mask24", 24, BF), ("mask24a", 24, BF), ("on", 1120, BF), ("tt", 512, BF), ("lt", 608, BF), ("ahl", 512, BF),
+        ("ao", 512, BF), ("a3", 512, BF), ("f3", 512, BF), ("f5", 512, BF), ("wtl", 512, BF), ("mk", 16, BF),
+        ("mh", 512, BF), ("ml", 512, BF), ("vt", 1664, BF), ("left", 1664, BF), ("at", 512, BF), ("left2", 512, BF),
+        ("d16", 128, BF), ("sm1", 128, BF), ("sm2", 128, BF), ("sm", 128, BF), ("thr3", 96, BF), ("thr3a", 96, BF), ("thr6", 6, BF), ("thr6a", 6, BF),
+        ("icol", 8, I32), ("ci", 8, F32), ("cf", 16, F32), ("pos", 24, F32), ("posc", 24, F32), ("mcb", 6, F32), ("mc", 6, F32),
+        ("sa", 8, F32), ("inc", 8, F32), ("z", 384, F32), ("ss", 384, F32), ("z2", 96, F32), ("ss2", 96, F32),
+        ("sc", 128, F32), ("sc2", 32, F32), ("mn", 24, F32), ("pu", 6, F32), ("pl", 6, F32), ("et", 24, F32), ("et2", 12, F32),
+        ("ysb", 128, F32), ("nbs", 4, F32),
+        ("ofs", 12, U16), ("ofd", 32, U16), ("ofp", 6, U16), ("ofw", 4, U16), ("ofe", 24, U16), ("ofo", 6, U16)):
+    SCRATCH[_n] = ("sbuf", [128, _w], _d)
+for _n, _w in (("erq", 384), ("eq", 512), ("uq", 128), ("onq", 280), ("ttq", 128), ("ttr", 128), ("ahlq", 128), ("aoq", 128),
+               ("a3q", 128), ("f3q", 128), ("f5q", 128), ("mhq", 128), ("mlq", 128), ("wq", 128), ("qb", 1184), ("send", 336),
+               ("land0", 176), ("land1", 176), ("land2", 176), ("den", 512), ("pw", 256), ("pb", 384), ("ws", 48),
+               ("wl", 168), ("oe", 480)):
+    SCRATCH[_n + "c"] = ("sbuf", [128, _w], CODE)
+    SCRATCH[_n + "s"] = ("sbuf", [128, _w], PLANE)
+SEMAPHORES = ["qv", "qa", "qt", "qg", "ls", "arr0", "arr1", "arr2", "arw0", "arw1", "arw2"] + ["d%d" % _i for _i in range(24)]
+
+
+def rank_program(g, core, T, topo):
+    rk = T.rank_of(core)
+    if rk is None:
+        return
+    A_, F_ = AluOpType, ActivationFunctionType
+    QUEUE = {"v": g.vector, "a": g.scalar, "t": g.tensor, "g": g, "s": g.sync}
+    own = [(rk + 1 + k) % N for k in range(N)]
+
+    known = {q: {} for q in QUEUE}
+    count = {"v": 0, "a": 0, "t": 0, "g": 0}
+    hist, ndma, dma_tok = {}, [0], []
+
+    def V(name, c0, c1, step=1, p0=0, p1=128):
+        return (name, c0, c1, step, p0, p1)
+
+    def PS(bank, c0, c1, step=1, p0=0, p1=128):
+        return ("ps", 512 * bank + c0, 512 * bank + c1, step, p0, p1)
+
+    def ap(v):
+        return T[v[0]][v[4]:v[5], v[1]:v[2]] if v[3] == 1 else T[v[0]][v[4]:v[5], v[1]:v[2]:v[3]]
+
+    def meet(a, b, one):
+        if a[0] == "ps" and not one:
+            return a[1] // 512 == b[1] // 512
+        if a[1] >= b[2] or b[1] >= a[2] or a[4] >= b[5] or b[4] >= a[5]:
+            return False
+        return not (a[3] == b[3] and a[3] > 1 and (a[1] - b[1]) % a[3])
+
+    def wait(q, toks):
+        for s, v, c in sorted(toks, key=lambda x: -len(x[2])):
+            if known[q].get(s, 0) >= v:
+                continue
+            if any(o[2].get(s, 0) >= v for o in toks if (o[0], o[1]) != (s, v) and known[q].get(o[0], 0) < o[1]):
+                continue
+            QUEUE[q].wait_ge(T.sem[s], v)
+            for k2, v2 in c.items():
+                known[q][k2] = max(known[q].get(k2, 0), v2)
+            known[q][s] = v
+
+    def need(q, outs, ins, who):
+        toks = {}
+        for v in ins:
+            for (w, tok, by, x) in hist.get(v[0], []):
+                if meet(v, x, by == who) and (w or (v[0] == "ps" and by != who)):
+                    toks[tok[:2]] = tok
+        for v in outs:
+            for (w, tok, by, x) in hist.get(v[0], []):
+                if meet(v, x, by == who) and not (by == who == "t"):
+                    toks[tok[:2]] = tok
+        wait(q, list(toks.values()))
+
+    def note(tok, by, outs, ins):
+        for w, vs in ((True, outs), (False, ins)):
+            for v in vs:
+                hist.setdefault(v[0], []).append((w, tok, by, v))
+
+    def run(q, call, outs, ins):
+        need(q, outs, ins, q)
+        count[q] += 1
+        s = "q" + q
+        call().then_inc(T.sem[s], 1)
+        tok = (s, count[q], dict(known[q]))
+        tok[2][s] = count[q]
+        note(tok, q, outs, ins)
+
+    def dma(q, out, src, oap=None, iap=None):
+        i = ndma[0]
+        ndma[0] += 1
+        outs, ins = ([out] if out else []), ([src] if src else [])
+        need(q, outs, ins, "d%d" % i)
+        QUEUE[q].dma_start(oap if oap is not None else ap(out), iap if iap is not None else ap(src)).then_inc(T.sem["d%d" % i], 16)
+        tok = ("d%d" % i, 16, dict(known[q]))
+        note(tok, "d%d" % i, outs, ins)
+        dma_tok.append((q, tok))
+
+    def fill(v, x):
+        run("v", lambda: g.vector.memset(ap(v), x), [v], [])
+
+    def copy(o, i):
+        run("v", lambda: g.vector.tensor_copy(ap(o), ap(i)), [o], [i])
+
+    def tt(o, a, b, op):
+        run("v", lambda: g.vector.tensor_tensor(ap(o), ap(a), ap(b), op), [o], [a, b])
+
+    def ts(o, a, s1, op0, s2=None, op1=None):
+        sc = [s for s in (s1, s2) if isinstance(s, tuple)]
+        x1 = ap(s1) if isinstance(s1, tuple) else s1
+        x2 = ap(s2) if isinstance(s2, tuple) else s2
+        if op1 is None:
+            run("v", lambda: g.vector.tensor_scalar(ap(o), ap(a), x1, None, op0), [o], [a] + sc)
+        else:
+            run("v", lambda: g.vector.tensor_scalar(ap(o), ap(a), x1, x2, op0, op1), [o], [a] + sc)
+
+    def act(o, i, func=F_.Copy, bias=0.0, scale=1.0):
+        sc = [s for s in (bias, scale) if isinstance(s, tuple)]
+        b = ap(bias) if isinstance(bias, tuple) else bias
+        s = ap(scale) if isinstance(scale, tuple) else scale
+        run("a", lambda: g.scalar.activation(ap(o), ap(i), func, bias=b, scale=s), [o], [i] + sc)
+
+    def zero(name, c0, c1):
+        act(V(name, c0, c1), V("zt", 0, c1 - c0))
+
+    def quant(name, c0, n, src, s0):
+        o, os, i = V(name + "c", c0, c0 + n), V(name + "s", c0, c0 + n), V(src, s0, s0 + 4 * n)
+        run("v", lambda: g.vector.quantize_mx(ap(o), ap(os), ap(i)), [o, os], [i])
+
+    def mm(bank, n, l, l0, r, r0, start=True, stop=True):
+        o = PS(bank, 0, n)
+        a, b = V(l + "c", l0, l0 + 128), V(l + "s", l0, l0 + 128)
+        c, d = V(r + "c", r0, r0 + n), V(r + "s", r0, r0 + n)
+        run("t", lambda: g.tensor.matmul_mx(ap(o), ap(a), ap(b), ap(c), ap(d), start, stop), [o], [a, b, c, d])
+
+    def pick(o, o0, w, w0, w1, off, k0, k1):
+        n, f = 16 * (k1 - k0), V(off, k0, k1)
+        a, b = V(o + "c", o0, o0 + n), V(w + "c", w0, w1)
+        run("v", lambda: g.vector.tensor_copy(ap(a).bitcast(dt.uint32), ap(b).bitcast(dt.uint32).indirect(ap(f))), [a], [b, f])
+        c, d = V(o + "s", o0, o0 + n), V(w + "s", w0, w1)
+        run("a", lambda: g.scalar.activation(ap(c), ap(d).indirect(ap(f)), F_.Copy), [c], [d, f])
+
+    def scan(o, n, bank):
+        run("v", lambda: g.vector.tensor_tensor_scan(ap(V(o, 0, n)), ap(V("sm", 0, n)), ap(PS(bank, 0, n)), 0.0, A_.add, A_.max),
+            [V(o, 0, n)], [V("sm", 0, n), PS(bank, 0, n)])
+
+    def sel(o, i, pattern, op, fillv, base, cm):
+        run("g", lambda: g.affine_select(ap(o), ap(i), pattern, op, fillv, base, cm), [o], [i])
+
+    def iota(o, pattern, base, cm, small=True):
+        if small:
+            run("g", lambda: g.iota(ap(o), pattern, base, cm, allow_small_or_imprecise_dtypes=True), [o], [])
+        else:
+            run("g", lambda: g.iota(ap(o), pattern, base, cm), [o], [])
+
+    def lo(name, c0, c1, step=1):
+        return V(name, c0, c1, step, 0, 96)
+
+    def hi(name, c0, c1, step=1):
+        return V(name, c0, c1, step, 96, 128)
+
+    dma("s", V("ert", 0, 768), None, iap=T.er[:, 0:768])
+    dma("a", V("uc", 0, 4), None, iap=T.u[:, 0:4])
+    dma("s", V("ert", 768, 1536), None, iap=T.er[:, 768:1536])
+    dma("a", V("grt", 0, 1536), None, iap=T.gr[:, :])
+    dma("s", V("fot", 0, 384), None, iap=T.fo[:, :])
+    dma("s", V("wt", 0, 512), None, iap=T.w[:, :])
+
+    fill(V("one", 0, 512), 1.0)
+    fill(V("ew", 0, 520), 0.0)
+    fill(V("zt", 0, 608), 0.0)
+    sel(V("ew", 3, 515, 4), V("one", 0, 128), [[-1, 128]], A_.is_equal, 0.0, 0, 1)
+    iota(V("icol", 0, 1), [[0, 1]], 0, 1, small=False)
+    iota(V("s16", 0, 128), [[0, 8], [1, 16]], 0, 0)
+    iota(V("hh", 0, 128), [[0, 4], [1, 2], [0, 16]], 0, 0)
+    sel(V("tri", 0, 96), V("one", 0, 96), [[1, 96]], A_.is_gt, 0.0, 0, -1)
+    sel(lo("on", 0, 512), lo("one", 0, 512), [[1, 4], [0, 32], [-1, 4]], A_.is_equal, 0.0, 0, 0)
+    sel(lo("on", 512, 608), lo("one", 0, 96), [[1, 4], [0, 6], [-1, 4]], A_.is_equal, 0.0, 0, 0)
+    sel(V("mask24a", 0, 24), V("one", 0, 24), [[0, 4], [-16, 6]], A_.is_ge, 0.0, 0, 1)
+    sel(V("mask24", 0, 24), V("mask24a", 0, 24), [[0, 4], [16, 6]], A_.is_ge, 0.0, 15, -1)
+
+    act(lo("tt", 0, 512), lo("zt", 0, 512))
+    zero("lt", 0, 608)
+    act(hi("on", 0, 608, 4), hi("zt", 0, 152))
+    for t in (1, 2, 3):
+        act(hi("on", t, 608, 4), hi("zt", 0, 152)) if t > 1 else act(hi("on", 513, 608, 4), hi("zt", 0, 24))
+    act(hi("on", 1, 512, 4), hi("s16", 0, 128), scale=-1.0 / 32)
+    zero("ahl", 0, 512)
+
+    for b in range(4):
+        quant("eq", 128 * b, 128, "ew", 3 - b)
+    for c, x in ((1, 15), (2, 7), (3, 3)):
+        ts(V("icol", c, c + 1), V("icol", 0, 1), x, A_.bitwise_and)
+    ts(V("icol", 4, 5), V("icol", 0, 1), 15, A_.bitwise_and, 2, A_.logical_shift_right)
+    ts(V("icol", 5, 6), V("icol", 0, 1), N - 1 - rk, A_.add)
+    ts(V("icol", 6, 7), V("icol", 5, 6), 3, A_.bitwise_and)
+    copy(V("ci", 0, 7), V("icol", 0, 7))
+    P0, P15, P7, P3, P42, PK = [V("ci", c, c + 1) for c in (0, 1, 2, 3, 4, 6)]
+    P8, CORR, XB10, XB8 = [V("cf", c, c + 1) for c in range(4)]
+    tt(P8, P0, P7, A_.subtract)
+    ts(CORR, P15, 15.0, A_.is_lt, 512.0, A_.mult)
+    ts(XB10, P15, 10.0, A_.subtract, 0.0, A_.max)
+    for k in range(4):
+        ts(V("ofs", 3 * k, 3 * k + 1), XB10, 640.0 + 6 * k, A_.add)
+    quant("qb", 192, 128, "zt", 0)
+    quant("qb", 320, 128, "zt", 0)
+    act(lo("ahl", 0, 512, 4), lo("one", 0, 128), scale=P8[:4] + (0, 96))
+    act(lo("ahl", 1, 512, 4), lo("one", 0, 128), scale=P7[:4] + (0, 96))
+    act(hi("ahl", 1, 512, 4), hi("one", 0, 128), scale=32.0)
+    act(V("ucf", 0, 4), V("uc", 0, 4))
+    for t in range(4):
+        act(V("urep", t, 512, 4), V("one", 0, 128), scale=V("ucf", t, t + 1))
+
+    quant("erq", 0, 192, "ert", 0)
+    quant("erq", 192, 192, "ert", 768)
+    for b in range(4):
+        mm(b, 384, "eq", 128 * b, "erq", 0)
+    quant("uq", 0, 128, "urep", 0)
+    act(hi("on", 0, 512, 4), hi("hh", 0, 128), scale=-0.5)
+    act(hi("on", 512, 608, 4), hi("one", 0, 24), scale=-0.5)
+    fill(hi("tt", 0, 512), 1.0)
+    for k, x in ((1, 3), (2, 7), (3, 10)):
+        fill(hi("lt", 128 * k + 1, 128 * k + 128, 4), x / 32)
+    fill(hi("lt", 513, 608, 4), 1.0)
+    for name in ("ao", "wtl", "f3"):
+        zero(name, 0, 512)
+    at0 = [0, 96, 224, 320]
+
+    def scale_s(c, bank):
+        act(lo("sa", c, c + 1), PS(bank, 0, 1, 1, 0, 96), F_.Abs)
+        act(lo("inc", c, c + 1), lo("sa", c, c + 1), F_.Identity, bias=2.0 ** -120, scale=1.25 * 2.0 ** -24)
+
+    RB, SB = (4, 7), (5, 6, 2, 3)
+
+    def add_v(b, k):
+        tt(V("vt", 4 * at0[k] + b, 4 * at0[k] + 384, 4), PS(b, own[k], 384, 4), V("grt", 4 * own[k] + b, 1536, 16), A_.add)
+
+    for b in range(3):
+        for k in range(4):
+            add_v(b, k)
+    for h in range(2):
+        for k in (2 * h, 2 * h + 1):
+            add_v(3, k)
+        quant("qb", at0[2 * h], 192, "vt", 4 * at0[2 * h])
+        mm(SB[2 * h], 128, "qb", at0[2 * h], "uq", 0)
+        mm(SB[2 * h + 1], 128, "qb", at0[2 * h + 1], "uq", 0)
+        mm(RB[h], 192, "uq", 0, "qb", at0[2 * h])
+    quant("onq", 0, 152, "on", 0)
+    ts(V("d16", 0, 128), V("s16", 0, 128), P15, A_.subtract)
+    ts(V("sm1", 0, 128), V("d16", 0, 128), 0.0, A_.is_equal, -4096.0, A_.mult)
+    for h in range(2):
+        for k in (2 * h, 2 * h + 1):
+            scale_s(k, SB[k])
+            if h == 0:
+                act(lo("ss", 96 * k, 96 * k + 96), lo("tri", 0, 96), F_.Identity, bias=lo("sa", k, k + 1), scale=lo("inc", k, k + 1))
+        for k in (2 * h, 2 * h + 1):
+            act(lo("z", 96 * k, 96 * k + 96), PS(RB[h], 96 * (k - 2 * h), 96 * (k - 2 * h) + 96, 1, 0, 96), F_.Abs)
+    for k in range(4):
+        if k == 2:
+            for k2 in (2, 3):
+                ts(lo("ss", 96 * k2, 96 * k2 + 96), lo("tri", 0, 96), lo("inc", k2, k2 + 1), A_.mult, lo("sa", k2, k2 + 1), A_.add)
+        tt(lo("tt", k, 384, 4), lo("z", 96 * k, 96 * k + 96), lo("ss", 96 * k, 96 * k + 96), A_.is_lt)
+    quant("ttq", 0, 128, "tt", 0)
+    mm(0, 152, "ttq", 0, "onq", 0)
+    quant("ahlq", 0, 128, "ahl", 0)
+    tt(lo("lt", 512, 608, 4), PS(0, 128, 152, 1, 0, 96), lo("mask24", 0, 24), A_.mult)
+    for t in range(2):
+        ts(lo("lt", t, 512, 4), PS(0, 0, 128, 1, 0, 96), 0.0, A_.is_equal)
+    quant("qb", 512, 152, "lt", 0)
+    ts(V("sm2", 0, 128), V("d16", 0, 128), 1.0, A_.is_equal, 512.0, A_.mult)
+    tt(V("sm", 0, 128), V("sm1", 0, 128), V("sm2", 0, 128), A_.add)
+    mm(1, 128, "ahlq", 0, "qb", 512)
+    scan("sc", 128, 1)
+    ts(V("ofs", 1, 12, 3), V("sc", 15, 128, 32), CORR, A_.subtract)
+    ts(V("ofs", 2, 12, 3), V("sc", 31, 128, 32), CORR, A_.subtract)
+    pick("send", 16, "qb", 0, 664, "ofs", 0, 12)
+
+    eng = topo.engines(core, T.cores[own[0]])
+    for k in range(3):
+        eng = [e for e in eng if e in topo.engines(core, T.cores[own[k]])]
+    q4 = len(eng) // 4
+    share = ([eng[0:2 * q4], eng[2 * q4:3 * q4], eng[3 * q4:4 * q4]],
+             [eng[2 * q4:4 * q4], eng[0:q4], eng[q4:2 * q4]])
+
+    def send(src, cols, dst, dcol, width, sem):
+        for part in (0, 1):
+            views, trs = [], []
+            for k in range(3):
+                m = 0
+                for e in share[part][k]:
+                    m |= 1 << e
+                rid, pid = topo.addr(T.cores[own[k]])[0:2]
+                sv = V(src + "cs"[part], cols[k], cols[k] + width)
+                dv = V(dst[2 - k] + "cs"[part], dcol[2 - k], dcol[2 - k] + width)
+                s_, d_ = (ap(sv).bitcast(dt.uint8), ap(dv).bitcast(dt.uint8)) if part == 0 else (ap(sv), ap(dv))
+                views.append(sv)
+                trs.append(RemoteDMATransfer(dst_ids=[DstId(rid=rid, pnc=pid)], dma_engine_mask=m, remote_sem=T.sem[sem[2 - k]], src=s_, dst=d_))
+            need("g", [], views, "g")
+            g.remote_dma_fused(trs, local_sem=T.sem.ls)
+
+    arrive = [len(share[0][2 - x]) + len(share[1][2 - x]) for x in range(3)]
+    left_ = 2 * sum(arrive)
+    send("send", [26 + 48 * k for k in range(3)], ["land0", "land1", "land2"], [10] * 3, 38, ["arr0", "arr1", "arr2"])
+    for x in range(3):
+        note(("arr%d" % x, arrive[x], {}), "far", [V("land%dc" % x, 10, 48), V("land%ds" % x, 10, 48)], [])
+
+    fill(V("fot", 384, 512), 0.0)
+    quant("pw", 128, 128, "fot", 0)
+    for b in range(4):
+        mm(4 + b, 128, "eq", 128 * b, "pw", 128, True, False)
+    for b in range(4):
+        mm(b, 416, "eq", 128 * b, "qb", 0)
+    quant("send", 208, 128, "zt", 0)
+    for x in range(3):
+        quant("land%d" % x, 48, 128, "zt", 0)
+    ts(lo("ao", 0, 512, 4), lo("s16", 0, 128), P15[:4] + (0, 96), A_.is_equal)
+    fill(hi("ao", 1, 512, 4), 1.0)
+    quant("aoq", 0, 128, "ao", 0)
+    fill(V("vt", 768, 896), 0.0)
+    fill(V("at", 384, 512), 0.0)
+    for s in range(4):
+        fill(V("ofd", 8 * s + 6, 8 * s + 8), 48)
+    for b in range(4):
+        tt(V("left", b, 1664, 4), V("vt", b, 1664, 4), PS(b, 0, 416), A_.subtract)
+    iota(V("mcb", 0, 6), [[16, 6]], 0, 0)
+    iota(V("pos", 0, 24), [[4, 24]], 0, 0)
+    sel(V("mk", 0, 16), V("one", 0, 16), [[1, 4], [-1, 4]], A_.is_equal, 0.0, 0, 0)
+    for name in ("mh", "ml"):
+        iota(V(name, 0, 512), [[0, 512]], 0, 0)
+    sel(lo("on", 608, 992), lo("one", 0, 384), [[0, 24], [1, 4], [-1, 4]], A_.is_equal, 0.0, 0, 0)
+    sel(V("thr3a", 0, 96), V("zt", 0, 96), [[-4, 24], [0, 4]], A_.is_ge, -1000.0, 0, 1)
+    sel(V("thr3", 0, 96), V("thr3a", 0, 96), [[4, 24], [0, 4]], A_.is_ge, -1000.0, 3, -1)
+    sel(V("thr6a", 0, 6), V("zt", 0, 6), [[-16, 6]], A_.is_ge, -1000.0, 0, 1)
+    sel(V("thr6", 0, 6), V("thr6a", 0, 6), [[16, 6]], A_.is_ge, -1000.0, 15, -1)
+    for name in ("a3", "f5"):
+        zero(name, 0, 512)
+    act(V("mc", 0, 6), V("mcb", 0, 6), F_.Identity, bias=P15)
+    act(hi("wtl", 128, 160), hi("one", 0, 32), scale=rk / 32.0)
+    ts(XB8, P15, 8.0, A_.subtract, 0.0, A_.max)
+    ts(V("ofw", 0, 1), XB8, 288.0, A_.add)
+    quant("pb", 0, 128, "zt", 0)
+
+    def place(s):
+        return ("send", 160) if s == rk else ("land%d" % ((s - rk - 1) % N), 0)
+
+    def offsets(s):
+        mm(s, 128, "aoq", 0, place(s)[0], place(s)[1] + 10)
+
+    def add(s):
+        for b in range(4):
+            mm(4 + b, 128, "eq", 128 * b, "den", 128 * s, False, s == N - 1)
+
+    offsets(0)
+    for s in range(4):
+        if s < 3:
+            offsets(s + 1)
+        copy(V("ofd", 8 * s, 8 * s + 6), PS(s, 0, 6))
+        w, c = place(s)
+        pick("den", 128 * s, w, c, c + 176, "ofd", 8 * s, 8 * s + 8)
+        add(s)
+    copy(V("mn", 0, 6), PS(0, 0, 6))
+    for s in range(1, 4):
+        tt(V("mn", 6 * s, 6 * s + 6), PS(s, 0, 6), V("mn", 6 * s - 6, 6 * s), A_.min)
+    ts(V("pu", 0, 6), V("mn", 18, 24), 48.0, A_.is_ge, 128.0, A_.mult)
+    tt(V("pl", 0, 6), V("pu", 0, 6), V("mc", 0, 6), A_.add)
+    copy(V("ofp", 0, 6), V("pl", 0, 6))
+    ts(V("cf", 4, 5), PK, 2.0, A_.is_ge, 32.0, A_.mult)
+    ts(V("cf", 5, 6), PK, 96.0, A_.mult, V("cf", 4, 5), A_.add)
+    ts(V("posc", 0, 24), V("pos", 0, 24), V("cf", 5, 6), A_.add, P42, A_.add)
+    for b in range(4):
+        o, i = V("at", b, 384, 4), PS(4 + b, 0, 96)
+        if b % 2:
+            act(o, i)
+        else:
+            copy(o, i)
+    quant("pw", 0, 128, "at", 0)
+    pick("pb", 0, "pw", 0, 256, "ofp", 0, 6)
+    mm(1, 128, "pb", 0, "uq", 0)
+    mm(0, 128, "uq", 0, "pb", 0)
+    scale_s(4, 1)
+    act(lo("ss2", 0, 96), lo("tri", 0, 96), F_.Identity, bias=lo("sa", 4, 5), scale=lo("inc", 4, 5))
+    act(lo("z2", 0, 96), PS(0, 0, 96, 1, 0, 96), F_.Abs)
+    for k in range(4):
+        ts(V("cf", 8 + k, 9 + k), P3, 4.0, A_.mult, float(own[k]), A_.add)
+    for k in range(4):
+        ts(lo("a3", k, 512, 4), lo("s16", 0, 128), V("cf", 8 + k, 9 + k, 1, 0, 96), A_.is_equal, 768.0, A_.mult)
+    quant("a3q", 0, 128, "a3", 0)
+    tt(lo("tt", 0, 384, 4), lo("z2", 0, 96), lo("ss2", 0, 96), A_.is_lt)
+    quant("ttr", 0, 128, "tt", 0)
+    mm(2, 128, "ttr", 0, "onq", 0)
+    for t in range(2):
+        ts(lo("wtl", t, 128, 4), PS(2, 0, 32, 1, 0, 96), 0.0, A_.is_equal)
+    ts(lo("wtl", 128, 160), PS(2, 0, 32, 1, 0, 96), 0.0, A_.is_equal)
+    quant("pb", 256, 128, "wtl", 0)
+    mm(3, 128, "ahlq", 0, "pb", 256)
+    scan("sc2", 32, 3)
+    ts(V("ofw", 1, 3), V("sc2", 15, 32, 16), CORR, A_.subtract)
+    pick("ws", 0, "pb", 0, 384, "ofw", 0, 3)
+    send("ws", [8] * 3, ["wl", "wl", "wl"], [48 + 40 * x for x in range(3)], 40, ["arw0", "arw1", "arw2"])
+    for x in range(3):
+        c0 = 48 + 40 * x
+        note(("arw%d" % x, arrive[x], {}), "far", [V("wlc", c0, c0 + 40), V("wls", c0, c0 + 40)], [])
+    pick("wl", 0, "pb", 0, 384, "ofw", 0, 3)
+
+    act(lo("on", 992, 1120), lo("zt", 0, 128))
+    for t in (1, 2, 3):
+        act(hi("on", 608 + t, 1120, 4), hi("zt", 0, 128))
+    act(hi("on", 992, 1120, 4), hi("zt", 0, 32))
+    act(hi("on", 608, 992, 4), hi("one", 0, 96), scale=-1.0)
+    zero("left2", 384, 512)
+    act(hi("ml", 0, 16), hi("mk", 0, 16))
+    for b in range(4):
+        mm(4 + b, 128, "eq", 128 * b, "pb", 0)
+    quant("qb", 768, 416, "left", 0)
+    quant("onq", 152, 128, "on", 608)
+    mm(0, 128, "ttq", 0, "onq", 152)
+    mm(2, 128, "ttr", 0, "onq", 152)
+    tt(lo("f3", 0, 96), PS(0, 0, 96, 1, 0, 96), lo("thr3", 0, 96), A_.is_lt)
+    quant("f3q", 0, 128, "f3", 0)
+    tt(lo("f5", 0, 24, 4), PS(2, 0, 24, 4, 0, 96), lo("thr6", 0, 6), A_.is_lt)
+    quant("f5q", 0, 128, "f5", 0)
+    mm(1, 128, "a3q", 0, "f3q", 0)
+    mm(3, 128, "aoq", 0, "f5q", 0)
+    tt(V("et", 0, 24), PS(1, 0, 24), V("posc", 0, 24), A_.add)
+    copy(V("ofe", 0, 24), V("et", 0, 24))
+    pick("oe", 0, "qb", 0, 1184, "ofe", 0, 24)
+    dma("s", None, V("oec", 0, 384), oap=T.oc[:, 0:1536], iap=T.oec[:, 0:384].bitcast(dt.uint8))
+    ts(V("et2", 0, 6), PS(3, 0, 6), 128.0, A_.mult)
+    tt(V("et2", 6, 12), V("et2", 0, 6), V("mc", 0, 6), A_.add)
+    copy(V("ofo", 0, 6), V("et2", 6, 12))
+    for b in range(4):
+        tt(V("left2", b, 384, 4), V("at", b, 384, 4), PS(4 + b, 0, 96), A_.subtract)
+    quant("pb", 128, 128, "left2", 0)
+    pick("oe", 384, "pb", 0, 256, "ofo", 0, 6)
+    dma("s", None, V("oec", 384, 480), oap=T.oc[:, 1536:1920], iap=T.oec[:, 384:480].bitcast(dt.uint8))
+    for k in range(4):
+        dma("s", None, V("oes", 0, 480, 1, 32 * k, 32 * k + 4), oap=T.osc[4 * k:4 * k + 4, :])
+    quant("wq", 0, 128, "wt", 0)
+    ts(V("cf", 6, 7), P8, 4.0, A_.mult)
+    ts(V("cf", 7, 8), P7, 4.0, A_.mult)
+    ts(lo("mh", 0, 16), lo("mk", 0, 16), V("cf", 6, 7, 1, 0, 96), A_.mult)
+    ts(lo("ml", 0, 16), lo("mk", 0, 16), V("cf", 7, 8, 1, 0, 96), A_.mult)
+    quant("mhq", 0, 128, "mh", 0)
+    quant("mlq", 0, 128, "ml", 0)
+
+    mm(4, 160, "wq", 0, "wl", 8)
+    mm(5, 128, "wl", 8, "mhq", 0, True, False)
+    mm(5, 128, "wl", 8, "mlq", 0, False, True)
+    order = [rk] + own[:3]
+    for b in range(4):
+        act(V("ysb", 32 * order[b], 32 * order[b] + 32), PS(4, 40 * b + 8, 40 * b + 40))
+    copy(V("nbs", 0, 4), PS(5, 0, 4))
+    dma("a", None, V("ysb", 0, 128), oap=T.y[:, :])
+    for b in range(4):
+        o = order[b]
+        dma("s", None, V("nbs", 0, 4, 1, 40 * b, 40 * b + 8), oap=T.nb[:, 32 * o:32 * o + 32])
+
+    g.wait_ge(T.sem.ls, left_)
+    for q, tok in dma_tok:
+        wait(q, [tok])
+    for q in ("v", "a", "t", "g"):
+        if known["s"].get("q" + q, 0) < count[q]:
+            g.sync.wait_ge(T.sem["q" + q], count[q])

@@ -3,17 +3,18 @@ from concourse.mybir import dt, AluOpType, ActivationFunctionType
 
 N, P, B, K = 4, 384, 96, 32
 F32, BF, I32, U16, CODE, PLANE = "float32", "bfloat16", "int32", "uint16", "float8_e4m3fn_x4", "uint8"
+STEP = 1.25 * 2.0 ** -24
 
 SCRATCH = {"ps": ("psum", [128, 4096], F32)}
 for _n, _w, _d in (
         ("ert", 1536, BF), ("grt", 1536, BF), ("fot", 512, BF), ("wt", 512, BF), ("uc", 4, BF), ("ucf", 4, F32),
-        ("one", 512, BF), ("zt", 608, BF), ("ew", 520, BF), ("urep", 512, BF), ("tri", 96, BF), ("s16", 128, BF),
+        ("one", 512, BF), ("cst", 96, BF), ("zt", 608, BF), ("ew", 520, BF), ("urep", 512, BF), ("tri", 96, BF), ("s16", 128, BF),
         ("hh", 128, BF), ("mask24", 24, BF), ("mask24a", 24, BF), ("on", 1120, BF), ("tt", 512, BF), ("lt", 608, BF), ("ahl", 512, BF),
         ("ao", 512, BF), ("a3", 512, BF), ("f3", 512, BF), ("f5", 512, BF), ("wtl", 512, BF), ("mk", 16, BF),
         ("mh", 512, BF), ("ml", 512, BF), ("vt", 1664, BF), ("left", 1664, BF), ("at", 512, BF), ("left2", 512, BF),
         ("d16", 128, BF), ("sm1", 128, BF), ("sm2", 128, BF), ("sm", 128, BF), ("thr3", 96, BF), ("thr3a", 96, BF), ("thr6", 6, BF), ("thr6a", 6, BF),
         ("icol", 8, I32), ("ci", 8, F32), ("cf", 16, F32), ("pos", 24, F32), ("posc", 24, F32), ("mcb", 6, F32), ("mc", 6, F32),
-        ("sa", 8, F32), ("inc", 8, F32), ("z", 384, F32), ("ss", 384, F32), ("z2", 96, F32), ("ss2", 96, F32),
+        ("sa", 8, F32), ("z", 384, F32), ("ss", 384, F32), ("z2", 96, F32), ("ss2", 96, F32),
         ("sc", 128, F32), ("sc2", 32, F32), ("mn", 24, F32), ("pu", 6, F32), ("pl", 6, F32), ("et", 24, F32), ("et2", 12, F32),
         ("ysb", 128, F32), ("nbs", 4, F32),
         ("ofs", 12, U16), ("ofd", 32, U16), ("ofp", 6, U16), ("ofw", 4, U16), ("ofe", 24, U16), ("ofo", 6, U16)):
@@ -166,20 +167,37 @@ def rank_program(g, core, T, topo):
         return V(name, c0, c1, step, 96, 128)
 
     dma("s", V("ert", 0, 768), None, iap=T.er[:, 0:768])
-    dma("a", V("uc", 0, 4), None, iap=T.u[:, 0:4])
     dma("s", V("ert", 768, 1536), None, iap=T.er[:, 768:1536])
-    dma("a", V("grt", 0, 1536), None, iap=T.gr[:, :])
+    dma("a", V("uc", 0, 4), None, iap=T.u[:, 0:4])
+    dma("s", V("grt", 0, 1536), None, iap=T.gr[:, :])
+    wait("s", [dma_tok[0][1], dma_tok[1][1]])
     dma("s", V("fot", 0, 384), None, iap=T.fo[:, :])
     dma("s", V("wt", 0, 512), None, iap=T.w[:, :])
 
-    fill(V("one", 0, 512), 1.0)
-    fill(V("ew", 0, 520), 0.0)
-    fill(V("zt", 0, 608), 0.0)
-    sel(V("ew", 3, 515, 4), V("one", 0, 128), [[-1, 128]], A_.is_equal, 0.0, 0, 1)
     iota(V("icol", 0, 1), [[0, 1]], 0, 1, small=False)
     iota(V("s16", 0, 128), [[0, 8], [1, 16]], 0, 0)
+    fill(V("one", 0, 512), 1.0)
+    fill(V("ew", 0, 520), 0.0)
+    sel(V("ew", 3, 515, 4), V("one", 0, 128), [[-1, 128]], A_.is_equal, 0.0, 0, 1)
+    fill(V("zt", 0, 608), 0.0)
+    for c, x in ((1, 15), (2, 7), (3, 3)):
+        ts(V("icol", c, c + 1), V("icol", 0, 1), x, A_.bitwise_and)
+    ts(V("icol", 5, 6), V("icol", 0, 1), N - 1 - rk, A_.add)
+    ts(V("icol", 4, 5), V("icol", 0, 1), 15, A_.bitwise_and, 2, A_.logical_shift_right)
+    quant("qb", 192, 128, "zt", 0)
+    ts(V("icol", 6, 7), V("icol", 5, 6), 3, A_.bitwise_and)
+    quant("qb", 320, 128, "zt", 0)
+    for b in range(4):
+        quant("eq", 128 * b, 128, "ew", 3 - b)
+        if b == 0:
+            copy(V("ci", 0, 7), V("icol", 0, 7))
+    P0, P15, P7, P3, P42, PK = [V("ci", c, c + 1) for c in (0, 1, 2, 3, 4, 6)]
+    P8, CORR, XB10, XB8 = [V("cf", c, c + 1) for c in range(4)]
+    tt(P8, P0, P7, A_.subtract)
+    fill(V("cst", 0, 96), STEP)
+
     iota(V("hh", 0, 128), [[0, 4], [1, 2], [0, 16]], 0, 0)
-    sel(V("tri", 0, 96), V("one", 0, 96), [[1, 96]], A_.is_gt, 0.0, 0, -1)
+    sel(V("tri", 0, 96), V("cst", 0, 96), [[1, 96]], A_.is_gt, 0.0, 0, -1)
     sel(lo("on", 0, 512), lo("one", 0, 512), [[1, 4], [0, 32], [-1, 4]], A_.is_equal, 0.0, 0, 0)
     sel(lo("on", 512, 608), lo("one", 0, 96), [[1, 4], [0, 6], [-1, 4]], A_.is_equal, 0.0, 0, 0)
     sel(V("mask24a", 0, 24), V("one", 0, 24), [[0, 4], [-16, 6]], A_.is_ge, 0.0, 0, 1)
@@ -187,85 +205,70 @@ def rank_program(g, core, T, topo):
 
     act(lo("tt", 0, 512), lo("zt", 0, 512))
     zero("lt", 0, 608)
-    act(hi("on", 0, 608, 4), hi("zt", 0, 152))
-    for t in (1, 2, 3):
-        act(hi("on", t, 608, 4), hi("zt", 0, 152)) if t > 1 else act(hi("on", 513, 608, 4), hi("zt", 0, 24))
-    act(hi("on", 1, 512, 4), hi("s16", 0, 128), scale=-1.0 / 32)
     zero("ahl", 0, 512)
-
-    for b in range(4):
-        quant("eq", 128 * b, 128, "ew", 3 - b)
-    for c, x in ((1, 15), (2, 7), (3, 3)):
-        ts(V("icol", c, c + 1), V("icol", 0, 1), x, A_.bitwise_and)
-    ts(V("icol", 4, 5), V("icol", 0, 1), 15, A_.bitwise_and, 2, A_.logical_shift_right)
-    ts(V("icol", 5, 6), V("icol", 0, 1), N - 1 - rk, A_.add)
-    ts(V("icol", 6, 7), V("icol", 5, 6), 3, A_.bitwise_and)
-    copy(V("ci", 0, 7), V("icol", 0, 7))
-    P0, P15, P7, P3, P42, PK = [V("ci", c, c + 1) for c in (0, 1, 2, 3, 4, 6)]
-    P8, CORR, XB10, XB8 = [V("cf", c, c + 1) for c in range(4)]
-    tt(P8, P0, P7, A_.subtract)
-    ts(CORR, P15, 15.0, A_.is_lt, 512.0, A_.mult)
-    ts(XB10, P15, 10.0, A_.subtract, 0.0, A_.max)
-    for k in range(4):
-        ts(V("ofs", 3 * k, 3 * k + 1), XB10, 640.0 + 6 * k, A_.add)
-    quant("qb", 192, 128, "zt", 0)
-    quant("qb", 320, 128, "zt", 0)
     act(lo("ahl", 0, 512, 4), lo("one", 0, 128), scale=P8[:4] + (0, 96))
     act(lo("ahl", 1, 512, 4), lo("one", 0, 128), scale=P7[:4] + (0, 96))
     act(hi("ahl", 1, 512, 4), hi("one", 0, 128), scale=32.0)
     act(V("ucf", 0, 4), V("uc", 0, 4))
     for t in range(4):
         act(V("urep", t, 512, 4), V("one", 0, 128), scale=V("ucf", t, t + 1))
+    act(hi("on", 513, 608, 4), hi("zt", 0, 24))
+    for t in (2, 3):
+        act(hi("on", t, 608, 4), hi("zt", 0, 152))
+    act(hi("on", 1, 512, 4), hi("s16", 0, 128), scale=-1.0 / 32)
+    act(hi("on", 0, 512, 4), hi("hh", 0, 128), scale=-0.5)
+    act(hi("on", 512, 608, 4), hi("one", 0, 24), scale=-0.5)
 
     quant("erq", 0, 192, "ert", 0)
     quant("erq", 192, 192, "ert", 768)
     for b in range(4):
         mm(b, 384, "eq", 128 * b, "erq", 0)
+    ts(CORR, P15, 15.0, A_.is_lt, 512.0, A_.mult)
+    ts(XB10, P15, 10.0, A_.subtract, 0.0, A_.max)
+    ts(V("d16", 0, 128), V("s16", 0, 128), P15, A_.subtract)
     quant("uq", 0, 128, "urep", 0)
-    act(hi("on", 0, 512, 4), hi("hh", 0, 128), scale=-0.5)
-    act(hi("on", 512, 608, 4), hi("one", 0, 24), scale=-0.5)
-    fill(hi("tt", 0, 512), 1.0)
-    for k, x in ((1, 3), (2, 7), (3, 10)):
-        fill(hi("lt", 128 * k + 1, 128 * k + 128, 4), x / 32)
-    fill(hi("lt", 513, 608, 4), 1.0)
+    ts(V("sm1", 0, 128), V("d16", 0, 128), 0.0, A_.is_equal, -4096.0, A_.mult)
+    ts(V("sm2", 0, 128), V("d16", 0, 128), 1.0, A_.is_equal, 512.0, A_.mult)
     for name in ("ao", "wtl", "f3"):
         zero(name, 0, 512)
     at0 = [0, 96, 224, 320]
 
-    def scale_s(c, bank):
-        act(lo("sa", c, c + 1), PS(bank, 0, 1, 1, 0, 96), F_.Abs)
-        act(lo("inc", c, c + 1), lo("sa", c, c + 1), F_.Identity, bias=2.0 ** -120, scale=1.25 * 2.0 ** -24)
+    def score(c, bank, src):
+        act(lo("sa", c, c + 1), PS(bank, 0, 1, 1, 0, 96), F_.Identity, bias=2.0 ** -87, scale=2.0 ** 30)
+
+    def raised(o, c0, c):
+        act(lo(o, c0, c0 + 96), lo("tri", 0, 96), F_.Abs, bias=lo("sa", c, c + 1), scale=lo("sa", c, c + 1))
+
+    def sizes(o, c0, n, bank):
+        act(lo(o, c0, c0 + n), PS(bank, 0, n, 1, 0, 96), F_.Abs, bias=V("cf", 15, 16, 1, 0, 96), scale=2.0 ** 30)
 
     RB, SB = (4, 7), (5, 6, 2, 3)
-
-    def add_v(b, k):
-        tt(V("vt", 4 * at0[k] + b, 4 * at0[k] + 384, 4), PS(b, own[k], 384, 4), V("grt", 4 * own[k] + b, 1536, 16), A_.add)
-
-    for b in range(3):
+    fill(V("cf", 15, 16), 2.0 ** -87)
+    for b in range(4):
         for k in range(4):
-            add_v(b, k)
+            tt(V("vt", 4 * at0[k] + b, 4 * at0[k] + 384, 4), PS(b, own[k], 384, 4), V("grt", 4 * own[k] + b, 1536, 16), A_.add)
     for h in range(2):
-        for k in (2 * h, 2 * h + 1):
-            add_v(3, k)
         quant("qb", at0[2 * h], 192, "vt", 4 * at0[2 * h])
         mm(SB[2 * h], 128, "qb", at0[2 * h], "uq", 0)
         mm(SB[2 * h + 1], 128, "qb", at0[2 * h + 1], "uq", 0)
         mm(RB[h], 192, "uq", 0, "qb", at0[2 * h])
+    fill(hi("tt", 0, 512), 1.0)
+    for k in range(4):
+        ts(V("ofs", 3 * k, 3 * k + 1), XB10, 640.0 + 6 * k, A_.add)
+    tt(V("sm", 0, 128), V("sm1", 0, 128), V("sm2", 0, 128), A_.add)
     quant("onq", 0, 152, "on", 0)
-    ts(V("d16", 0, 128), V("s16", 0, 128), P15, A_.subtract)
-    ts(V("sm1", 0, 128), V("d16", 0, 128), 0.0, A_.is_equal, -4096.0, A_.mult)
     for h in range(2):
         for k in (2 * h, 2 * h + 1):
-            scale_s(k, SB[k])
-            if h == 0:
-                act(lo("ss", 96 * k, 96 * k + 96), lo("tri", 0, 96), F_.Identity, bias=lo("sa", k, k + 1), scale=lo("inc", k, k + 1))
+            score(k, SB[k], None)
         for k in (2 * h, 2 * h + 1):
-            act(lo("z", 96 * k, 96 * k + 96), PS(RB[h], 96 * (k - 2 * h), 96 * (k - 2 * h) + 96, 1, 0, 96), F_.Abs)
+            raised("ss", 96 * k, k)
+        sizes("z", 192 * h, 192, RB[h])
     for k in range(4):
-        if k == 2:
-            for k2 in (2, 3):
-                ts(lo("ss", 96 * k2, 96 * k2 + 96), lo("tri", 0, 96), lo("inc", k2, k2 + 1), A_.mult, lo("sa", k2, k2 + 1), A_.add)
         tt(lo("tt", k, 384, 4), lo("z", 96 * k, 96 * k + 96), lo("ss", 96 * k, 96 * k + 96), A_.is_lt)
+        if k == 1:
+            for k2, x in ((1, 3), (2, 7), (3, 10)):
+                fill(hi("lt", 128 * k2 + 1, 128 * k2 + 128, 4), x / 32)
+            fill(hi("lt", 513, 608, 4), 1.0)
     quant("ttq", 0, 128, "tt", 0)
     mm(0, 152, "ttq", 0, "onq", 0)
     quant("ahlq", 0, 128, "ahl", 0)
@@ -273,13 +276,14 @@ def rank_program(g, core, T, topo):
     for t in range(2):
         ts(lo("lt", t, 512, 4), PS(0, 0, 128, 1, 0, 96), 0.0, A_.is_equal)
     quant("qb", 512, 152, "lt", 0)
-    ts(V("sm2", 0, 128), V("d16", 0, 128), 1.0, A_.is_equal, 512.0, A_.mult)
-    tt(V("sm", 0, 128), V("sm1", 0, 128), V("sm2", 0, 128), A_.add)
     mm(1, 128, "ahlq", 0, "qb", 512)
+    ts(XB8, P15, 8.0, A_.subtract, 0.0, A_.max)
+    fill(V("fot", 384, 512), 0.0)
     scan("sc", 128, 1)
     ts(V("ofs", 1, 12, 3), V("sc", 15, 128, 32), CORR, A_.subtract)
     ts(V("ofs", 2, 12, 3), V("sc", 31, 128, 32), CORR, A_.subtract)
-    pick("send", 16, "qb", 0, 664, "ofs", 0, 12)
+    pick("send", 16, "qb", 0, 664, "ofs", 0, 8)
+    pick("send", 144, "qb", 0, 664, "ofs", 8, 12)
 
     eng = topo.engines(core, T.cores[own[0]])
     for k in range(3):
@@ -310,40 +314,36 @@ def rank_program(g, core, T, topo):
     for x in range(3):
         note(("arr%d" % x, arrive[x], {}), "far", [V("land%dc" % x, 10, 48), V("land%ds" % x, 10, 48)], [])
 
-    fill(V("fot", 384, 512), 0.0)
     quant("pw", 128, 128, "fot", 0)
     for b in range(4):
-        mm(4 + b, 128, "eq", 128 * b, "pw", 128, True, False)
-    for b in range(4):
         mm(b, 416, "eq", 128 * b, "qb", 0)
-    quant("send", 208, 128, "zt", 0)
-    for x in range(3):
-        quant("land%d" % x, 48, 128, "zt", 0)
+    for b in range(4):
+        mm(4 + b, 128, "eq", 128 * b, "pw", 128, True, False)
     ts(lo("ao", 0, 512, 4), lo("s16", 0, 128), P15[:4] + (0, 96), A_.is_equal)
     fill(hi("ao", 1, 512, 4), 1.0)
+    fill(V("ofd", 0, 32), 48)
+    quant("send", 208, 128, "zt", 0)
     quant("aoq", 0, 128, "ao", 0)
+    for x in range(3):
+        quant("land%d" % x, 48, 128, "zt", 0)
     fill(V("vt", 768, 896), 0.0)
     fill(V("at", 384, 512), 0.0)
-    for s in range(4):
-        fill(V("ofd", 8 * s + 6, 8 * s + 8), 48)
+    ts(V("ofw", 0, 1), XB8, 288.0, A_.add)
     for b in range(4):
         tt(V("left", b, 1664, 4), V("vt", b, 1664, 4), PS(b, 0, 416), A_.subtract)
     iota(V("mcb", 0, 6), [[16, 6]], 0, 0)
     iota(V("pos", 0, 24), [[4, 24]], 0, 0)
     sel(V("mk", 0, 16), V("one", 0, 16), [[1, 4], [-1, 4]], A_.is_equal, 0.0, 0, 0)
-    for name in ("mh", "ml"):
-        iota(V(name, 0, 512), [[0, 512]], 0, 0)
     sel(lo("on", 608, 992), lo("one", 0, 384), [[0, 24], [1, 4], [-1, 4]], A_.is_equal, 0.0, 0, 0)
     sel(V("thr3a", 0, 96), V("zt", 0, 96), [[-4, 24], [0, 4]], A_.is_ge, -1000.0, 0, 1)
-    sel(V("thr3", 0, 96), V("thr3a", 0, 96), [[4, 24], [0, 4]], A_.is_ge, -1000.0, 3, -1)
     sel(V("thr6a", 0, 6), V("zt", 0, 6), [[-16, 6]], A_.is_ge, -1000.0, 0, 1)
+    sel(V("thr3", 0, 96), V("thr3a", 0, 96), [[4, 24], [0, 4]], A_.is_ge, -1000.0, 3, -1)
     sel(V("thr6", 0, 6), V("thr6a", 0, 6), [[16, 6]], A_.is_ge, -1000.0, 15, -1)
-    for name in ("a3", "f5"):
-        zero(name, 0, 512)
     act(V("mc", 0, 6), V("mcb", 0, 6), F_.Identity, bias=P15)
     act(hi("wtl", 128, 160), hi("one", 0, 32), scale=rk / 32.0)
-    ts(XB8, P15, 8.0, A_.subtract, 0.0, A_.max)
-    ts(V("ofw", 0, 1), XB8, 288.0, A_.add)
+    for name in ("mh", "ml", "a3"):
+        zero(name, 0, 512)
+    act(hi("ml", 0, 16), hi("mk", 0, 16))
     quant("pb", 0, 128, "zt", 0)
 
     def place(s):
@@ -361,18 +361,18 @@ def rank_program(g, core, T, topo):
         if s < 3:
             offsets(s + 1)
         copy(V("ofd", 8 * s, 8 * s + 6), PS(s, 0, 6))
+        if s == 0:
+            copy(V("mn", 0, 6), PS(0, 0, 6))
+        else:
+            tt(V("mn", 6 * s, 6 * s + 6), PS(s, 0, 6), V("mn", 6 * s - 6, 6 * s), A_.min)
         w, c = place(s)
         pick("den", 128 * s, w, c, c + 176, "ofd", 8 * s, 8 * s + 8)
         add(s)
-    copy(V("mn", 0, 6), PS(0, 0, 6))
-    for s in range(1, 4):
-        tt(V("mn", 6 * s, 6 * s + 6), PS(s, 0, 6), V("mn", 6 * s - 6, 6 * s), A_.min)
     ts(V("pu", 0, 6), V("mn", 18, 24), 48.0, A_.is_ge, 128.0, A_.mult)
-    tt(V("pl", 0, 6), V("pu", 0, 6), V("mc", 0, 6), A_.add)
-    copy(V("ofp", 0, 6), V("pl", 0, 6))
     ts(V("cf", 4, 5), PK, 2.0, A_.is_ge, 32.0, A_.mult)
-    ts(V("cf", 5, 6), PK, 96.0, A_.mult, V("cf", 4, 5), A_.add)
-    ts(V("posc", 0, 24), V("pos", 0, 24), V("cf", 5, 6), A_.add, P42, A_.add)
+    tt(V("pl", 0, 6), V("pu", 0, 6), V("mc", 0, 6), A_.add)
+    ts(V("cf", 6, 7), P8, 4.0, A_.mult)
+    copy(V("ofp", 0, 6), V("pl", 0, 6))
     for b in range(4):
         o, i = V("at", b, 384, 4), PS(4 + b, 0, 96)
         if b % 2:
@@ -383,22 +383,28 @@ def rank_program(g, core, T, topo):
     pick("pb", 0, "pw", 0, 256, "ofp", 0, 6)
     mm(1, 128, "pb", 0, "uq", 0)
     mm(0, 128, "uq", 0, "pb", 0)
-    scale_s(4, 1)
-    act(lo("ss2", 0, 96), lo("tri", 0, 96), F_.Identity, bias=lo("sa", 4, 5), scale=lo("inc", 4, 5))
-    act(lo("z2", 0, 96), PS(0, 0, 96, 1, 0, 96), F_.Abs)
+    score(4, 1, None)
+    raised("ss2", 0, 4)
+    sizes("z2", 0, 96, 0)
+    ts(V("cf", 5, 6), PK, 96.0, A_.mult, V("cf", 4, 5), A_.add)
+    ts(V("cf", 7, 8), P7, 4.0, A_.mult)
     for k in range(4):
         ts(V("cf", 8 + k, 9 + k), P3, 4.0, A_.mult, float(own[k]), A_.add)
+    ts(V("posc", 0, 24), V("pos", 0, 24), V("cf", 5, 6), A_.add, P42, A_.add)
     for k in range(4):
         ts(lo("a3", k, 512, 4), lo("s16", 0, 128), V("cf", 8 + k, 9 + k, 1, 0, 96), A_.is_equal, 768.0, A_.mult)
-    quant("a3q", 0, 128, "a3", 0)
     tt(lo("tt", 0, 384, 4), lo("z2", 0, 96), lo("ss2", 0, 96), A_.is_lt)
     quant("ttr", 0, 128, "tt", 0)
     mm(2, 128, "ttr", 0, "onq", 0)
+    quant("a3q", 0, 128, "a3", 0)
+    ts(lo("mh", 0, 16), lo("mk", 0, 16), V("cf", 6, 7, 1, 0, 96), A_.mult)
+    ts(lo("ml", 0, 16), lo("mk", 0, 16), V("cf", 7, 8, 1, 0, 96), A_.mult)
     for t in range(2):
         ts(lo("wtl", t, 128, 4), PS(2, 0, 32, 1, 0, 96), 0.0, A_.is_equal)
     ts(lo("wtl", 128, 160), PS(2, 0, 32, 1, 0, 96), 0.0, A_.is_equal)
     quant("pb", 256, 128, "wtl", 0)
     mm(3, 128, "ahlq", 0, "pb", 256)
+    quant("wq", 0, 128, "wt", 0)
     scan("sc2", 32, 3)
     ts(V("ofw", 1, 3), V("sc2", 15, 32, 16), CORR, A_.subtract)
     pick("ws", 0, "pb", 0, 384, "ofw", 0, 3)
@@ -414,40 +420,35 @@ def rank_program(g, core, T, topo):
     act(hi("on", 992, 1120, 4), hi("zt", 0, 32))
     act(hi("on", 608, 992, 4), hi("one", 0, 96), scale=-1.0)
     zero("left2", 384, 512)
-    act(hi("ml", 0, 16), hi("mk", 0, 16))
+    zero("f5", 0, 512)
     for b in range(4):
         mm(4 + b, 128, "eq", 128 * b, "pb", 0)
     quant("qb", 768, 416, "left", 0)
+    quant("mhq", 0, 128, "mh", 0)
+    quant("mlq", 0, 128, "ml", 0)
     quant("onq", 152, 128, "on", 608)
     mm(0, 128, "ttq", 0, "onq", 152)
     mm(2, 128, "ttr", 0, "onq", 152)
-    tt(lo("f3", 0, 96), PS(0, 0, 96, 1, 0, 96), lo("thr3", 0, 96), A_.is_lt)
-    quant("f3q", 0, 128, "f3", 0)
-    tt(lo("f5", 0, 24, 4), PS(2, 0, 24, 4, 0, 96), lo("thr6", 0, 6), A_.is_lt)
-    quant("f5q", 0, 128, "f5", 0)
-    mm(1, 128, "a3q", 0, "f3q", 0)
-    mm(3, 128, "aoq", 0, "f5q", 0)
-    tt(V("et", 0, 24), PS(1, 0, 24), V("posc", 0, 24), A_.add)
-    copy(V("ofe", 0, 24), V("et", 0, 24))
-    pick("oe", 0, "qb", 0, 1184, "ofe", 0, 24)
-    dma("s", None, V("oec", 0, 384), oap=T.oc[:, 0:1536], iap=T.oec[:, 0:384].bitcast(dt.uint8))
-    ts(V("et2", 0, 6), PS(3, 0, 6), 128.0, A_.mult)
-    tt(V("et2", 6, 12), V("et2", 0, 6), V("mc", 0, 6), A_.add)
-    copy(V("ofo", 0, 6), V("et2", 6, 12))
     for b in range(4):
         tt(V("left2", b, 384, 4), V("at", b, 384, 4), PS(4 + b, 0, 96), A_.subtract)
+    tt(lo("f3", 0, 96), PS(0, 0, 96, 1, 0, 96), lo("thr3", 0, 96), A_.is_lt)
+    tt(lo("f5", 0, 24, 4), PS(2, 0, 24, 4, 0, 96), lo("thr6", 0, 6), A_.is_lt)
+    quant("f3q", 0, 128, "f3", 0)
+    mm(1, 128, "a3q", 0, "f3q", 0)
+    quant("f5q", 0, 128, "f5", 0)
+    mm(3, 128, "aoq", 0, "f5q", 0)
     quant("pb", 128, 128, "left2", 0)
+    tt(V("et", 0, 24), PS(1, 0, 24), V("posc", 0, 24), A_.add)
+    ts(V("et2", 0, 6), PS(3, 0, 6), 128.0, A_.mult)
+    copy(V("ofe", 0, 24), V("et", 0, 24))
+    tt(V("et2", 6, 12), V("et2", 0, 6), V("mc", 0, 6), A_.add)
+    pick("oe", 0, "qb", 0, 1184, "ofe", 0, 24)
+    dma("s", None, V("oec", 0, 384), oap=T.oc[:, 0:1536], iap=T.oec[:, 0:384].bitcast(dt.uint8))
+    copy(V("ofo", 0, 6), V("et2", 6, 12))
     pick("oe", 384, "pb", 0, 256, "ofo", 0, 6)
     dma("s", None, V("oec", 384, 480), oap=T.oc[:, 1536:1920], iap=T.oec[:, 384:480].bitcast(dt.uint8))
     for k in range(4):
         dma("s", None, V("oes", 0, 480, 1, 32 * k, 32 * k + 4), oap=T.osc[4 * k:4 * k + 4, :])
-    quant("wq", 0, 128, "wt", 0)
-    ts(V("cf", 6, 7), P8, 4.0, A_.mult)
-    ts(V("cf", 7, 8), P7, 4.0, A_.mult)
-    ts(lo("mh", 0, 16), lo("mk", 0, 16), V("cf", 6, 7, 1, 0, 96), A_.mult)
-    ts(lo("ml", 0, 16), lo("mk", 0, 16), V("cf", 7, 8, 1, 0, 96), A_.mult)
-    quant("mhq", 0, 128, "mh", 0)
-    quant("mlq", 0, 128, "ml", 0)
 
     mm(4, 160, "wq", 0, "wl", 8)
     mm(5, 128, "wl", 8, "mhq", 0, True, False)

@@ -1,5 +1,5 @@
 from concourse.bass import DstId, RemoteDMATransfer
-from concourse.mybir import dt, AluOpType, ActivationFunctionType
+from concourse.mybir import dt, AluOpType, ActivationFunctionType, AxisListType
 
 N, P, B, K = 4, 384, 96, 32
 F32, BF, I32, U16, CODE, PLANE = "float32", "bfloat16", "int32", "uint16", "float8_e4m3fn_x4", "uint8"
@@ -13,19 +13,19 @@ for _n, _w, _d in (
         ("ao", 512, BF), ("a3", 512, BF), ("f3", 512, BF), ("f5", 512, BF), ("wtl", 512, BF), ("mk", 16, BF),
         ("mh", 512, BF), ("ml", 512, BF), ("vt", 1664, BF), ("left", 1664, BF), ("at", 512, BF), ("left2", 512, BF),
         ("d16", 128, BF), ("sm1", 128, BF), ("sm2", 128, BF), ("sm", 128, BF), ("thr3", 96, BF), ("thr3a", 96, BF), ("thr6", 6, BF), ("thr6a", 6, BF),
-        ("icol", 8, I32), ("ci", 8, F32), ("cf", 16, F32), ("pos", 24, F32), ("posc", 24, F32), ("mcb", 6, F32), ("mc", 6, F32),
-        ("sa", 8, F32), ("z", 384, F32), ("ss", 384, F32), ("z2", 96, F32), ("ss2", 96, F32),
-        ("sc", 128, F32), ("sc2", 32, F32), ("mn", 24, F32), ("pu", 6, F32), ("pl", 6, F32), ("et", 24, F32), ("et2", 12, F32),
+        ("icol", 8, I32), ("ci", 8, F32), ("cf", 16, F32), ("cg", 8, F32), ("k6", 4, F32), ("pos", 24, F32), ("posc", 24, F32), ("mcb", 6, F32), ("mc", 6, F32),
+        ("sa", 8, F32), ("z", 384, F32), ("ss", 384, F32), ("zw", 224, F32), ("ss2", 96, F32),
+        ("sc", 128, F32), ("sc2", 32, F32), ("mn", 24, F32), ("pu", 6, F32), ("pm", 6, F32), ("pl", 6, F32), ("et", 24, F32), ("et2", 12, F32),
         ("ysb", 128, F32), ("nbs", 4, F32),
-        ("ofs", 12, U16), ("ofd", 32, U16), ("ofp", 6, U16), ("ofw", 4, U16), ("ofe", 24, U16), ("ofo", 6, U16)):
+        ("ofs", 10, U16), ("ofo3", 4, U16), ("ofd", 32, U16), ("ofp", 6, U16), ("ofw", 4, U16), ("ofe", 24, U16), ("ofo", 6, U16)):
     SCRATCH[_n] = ("sbuf", [128, _w], _d)
-for _n, _w in (("erq", 384), ("eq", 512), ("uq", 128), ("onq", 280), ("ttq", 128), ("ttr", 128), ("ahlq", 128), ("aoq", 128),
-               ("a3q", 128), ("f3q", 128), ("f5q", 128), ("mhq", 128), ("mlq", 128), ("wq", 128), ("qb", 1184), ("send", 336),
+for _n, _w in (("erq", 384), ("eq", 512), ("uq", 128), ("zq", 128), ("onq", 280), ("ttq", 128), ("ttr", 128), ("ahlq", 128), ("aoq", 128),
+               ("a3q", 128), ("f3q", 128), ("f5q", 128), ("mhq", 128), ("mlq", 128), ("wq", 128), ("lq", 128), ("qb", 1184), ("send", 336),
                ("land0", 176), ("land1", 176), ("land2", 176), ("den", 512), ("pw", 256), ("pb", 384), ("ws", 48),
                ("wl", 168), ("oe", 480)):
     SCRATCH[_n + "c"] = ("sbuf", [128, _w], CODE)
     SCRATCH[_n + "s"] = ("sbuf", [128, _w], PLANE)
-SEMAPHORES = ["qv", "qa", "qt", "qg", "ls", "arr0", "arr1", "arr2", "arw0", "arw1", "arw2"] + ["d%d" % _i for _i in range(24)]
+SEMAPHORES = ["qv", "qa", "qt", "qg", "ls", "arr0", "arr1", "arr2", "arw0", "arw1", "arw2"] + ["d%d" % _i for _i in range(32)]
 
 
 def rank_program(g, core, T, topo):
@@ -109,8 +109,11 @@ def rank_program(g, core, T, topo):
     def copy(o, i):
         run("v", lambda: g.vector.tensor_copy(ap(o), ap(i)), [o], [i])
 
-    def tt(o, a, b, op):
-        run("v", lambda: g.vector.tensor_tensor(ap(o), ap(a), ap(b), op), [o], [a, b])
+    def tt(o, a, b, op, off=None):
+        if off is None:
+            run("v", lambda: g.vector.tensor_tensor(ap(o), ap(a), ap(b), op), [o], [a, b])
+        else:
+            run("v", lambda: g.vector.tensor_tensor(ap(o), ap(a).indirect(ap(off)), ap(b), op), [o], [a, b, off])
 
     def ts(o, a, s1, op0, s2=None, op1=None):
         sc = [s for s in (s1, s2) if isinstance(s, tuple)]
@@ -140,12 +143,19 @@ def rank_program(g, core, T, topo):
         c, d = V(r + "c", r0, r0 + n), V(r + "s", r0, r0 + n)
         run("t", lambda: g.tensor.matmul_mx(ap(o), ap(a), ap(b), ap(c), ap(d), start, stop), [o], [a, b, c, d])
 
-    def pick(o, o0, w, w0, w1, off, k0, k1):
+    def pick_codes(o, o0, w, w0, w1, off, k0, k1):
         n, f = 16 * (k1 - k0), V(off, k0, k1)
         a, b = V(o + "c", o0, o0 + n), V(w + "c", w0, w1)
         run("v", lambda: g.vector.tensor_copy(ap(a).bitcast(dt.uint32), ap(b).bitcast(dt.uint32).indirect(ap(f))), [a], [b, f])
+
+    def pick_scales(o, o0, w, w0, w1, off, k0, k1):
+        n, f = 16 * (k1 - k0), V(off, k0, k1)
         c, d = V(o + "s", o0, o0 + n), V(w + "s", w0, w1)
         run("a", lambda: g.scalar.activation(ap(c), ap(d).indirect(ap(f)), F_.Copy), [c], [d, f])
+
+    def pick(*a):
+        pick_codes(*a)
+        pick_scales(*a)
 
     def scan(o, n, bank):
         run("v", lambda: g.vector.tensor_tensor_scan(ap(V(o, 0, n)), ap(V("sm", 0, n)), ap(PS(bank, 0, n)), 0.0, A_.add, A_.max),
@@ -167,10 +177,10 @@ def rank_program(g, core, T, topo):
         return V(name, c0, c1, step, 96, 128)
 
     dma("s", V("ert", 0, 768), None, iap=T.er[:, 0:768])
-    dma("s", V("ert", 768, 1536), None, iap=T.er[:, 768:1536])
-    dma("a", V("uc", 0, 4), None, iap=T.u[:, 0:4])
+    dma("a", V("ert", 768, 1536), None, iap=T.er[:, 768:1536])
     dma("s", V("grt", 0, 1536), None, iap=T.gr[:, :])
-    wait("s", [dma_tok[0][1], dma_tok[1][1]])
+    dma("a", V("uc", 0, 4), None, iap=T.u[:, 0:4])
+    wait("s", [dma_tok[2][1]])
     dma("s", V("fot", 0, 384), None, iap=T.fo[:, :])
     dma("s", V("wt", 0, 512), None, iap=T.w[:, :])
 
@@ -184,106 +194,133 @@ def rank_program(g, core, T, topo):
         ts(V("icol", c, c + 1), V("icol", 0, 1), x, A_.bitwise_and)
     ts(V("icol", 5, 6), V("icol", 0, 1), N - 1 - rk, A_.add)
     ts(V("icol", 4, 5), V("icol", 0, 1), 15, A_.bitwise_and, 2, A_.logical_shift_right)
-    quant("qb", 192, 128, "zt", 0)
+    fill(V("cst", 0, 96), STEP)
     ts(V("icol", 6, 7), V("icol", 5, 6), 3, A_.bitwise_and)
-    quant("qb", 320, 128, "zt", 0)
+    quant("qb", 192, 128, "zt", 0)
+    P0, P15, P7, P3, P42, PK = [V("ci", c, c + 1) for c in (0, 1, 2, 3, 4, 6)]
+    P8, CORR, XB8, TINY = [V("cf", c, c + 1) for c in (0, 1, 3, 15)]
+    copy(V("ci", 0, 7), V("icol", 0, 7))
+    iota(V("hh", 0, 128), [[0, 4], [1, 2], [0, 16]], 0, 0)
+    iota(V("k6", 0, 4), [[6, 4]], 734, 0)
+    sel(V("tri", 0, 96), V("cst", 0, 96), [[1, 96]], A_.is_gt, 0.0, 0, -1)
     for b in range(4):
         quant("eq", 128 * b, 128, "ew", 3 - b)
         if b == 0:
-            copy(V("ci", 0, 7), V("icol", 0, 7))
-    P0, P15, P7, P3, P42, PK = [V("ci", c, c + 1) for c in (0, 1, 2, 3, 4, 6)]
-    P8, CORR, XB10, XB8 = [V("cf", c, c + 1) for c in range(4)]
-    tt(P8, P0, P7, A_.subtract)
-    fill(V("cst", 0, 96), STEP)
+            tt(P8, P0, P7, A_.subtract)
+            ts(V("d16", 0, 128), V("s16", 0, 128), P15, A_.subtract)
+            ts(CORR, P15, 15.0, A_.is_lt, 512.0, A_.mult)
+        if b == 1:
+            ts(V("sm1", 0, 128), V("d16", 0, 128), 0.0, A_.is_equal, -4096.0, A_.mult)
+            ts(V("sm2", 0, 128), V("d16", 0, 128), 1.0, A_.is_equal, 512.0, A_.mult)
+    quant("qb", 320, 128, "zt", 0)
+    quant("zq", 0, 128, "zt", 0)
+    for name, c, n in (("land0", 48, 90), ("land1", 48, 90), ("land2", 48, 90), ("send", 208, 90), ("pb", 96, 32)):
+        o, i = V(name + "c", c, c + n), V("zqc", 0, n)
+        dma("s", o, i, ap(o).bitcast(dt.uint8), ap(i).bitcast(dt.uint8))
+        dma("s", V(name + "s", c, c + n), V("zqs", 0, n))
+    fill(hi("tt", 0, 512), 1.0)
+    fill(TINY, 2.0 ** -87)
+    ts(V("ofs", 0, 9, 3), V("k6", 0, 3), P15, A_.add)
+    ts(V("ofo3", 0, 1), V("k6", 3, 4), P15, A_.add)
+    tt(V("sm", 0, 128), V("sm1", 0, 128), V("sm2", 0, 128), A_.add)
 
-    iota(V("hh", 0, 128), [[0, 4], [1, 2], [0, 16]], 0, 0)
-    sel(V("tri", 0, 96), V("cst", 0, 96), [[1, 96]], A_.is_gt, 0.0, 0, -1)
     sel(lo("on", 0, 512), lo("one", 0, 512), [[1, 4], [0, 32], [-1, 4]], A_.is_equal, 0.0, 0, 0)
     sel(lo("on", 512, 608), lo("one", 0, 96), [[1, 4], [0, 6], [-1, 4]], A_.is_equal, 0.0, 0, 0)
-    sel(V("mask24a", 0, 24), V("one", 0, 24), [[0, 4], [-16, 6]], A_.is_ge, 0.0, 0, 1)
-    sel(V("mask24", 0, 24), V("mask24a", 0, 24), [[0, 4], [16, 6]], A_.is_ge, 0.0, 15, -1)
+    iota(V("pos", 0, 24), [[4, 24]], 0, 0)
+    iota(V("mcb", 0, 6), [[16, 6]], 0, 0)
 
     act(lo("tt", 0, 512), lo("zt", 0, 512))
-    zero("lt", 0, 608)
     zero("ahl", 0, 512)
     act(lo("ahl", 0, 512, 4), lo("one", 0, 128), scale=P8[:4] + (0, 96))
     act(lo("ahl", 1, 512, 4), lo("one", 0, 128), scale=P7[:4] + (0, 96))
-    act(hi("ahl", 1, 512, 4), hi("one", 0, 128), scale=32.0)
+    act(hi("ahl", 1, 512, 4), hi("one", 0, 128))
     act(V("ucf", 0, 4), V("uc", 0, 4))
     for t in range(4):
         act(V("urep", t, 512, 4), V("one", 0, 128), scale=V("ucf", t, t + 1))
     act(hi("on", 513, 608, 4), hi("zt", 0, 24))
-    for t in (2, 3):
+    for t in (0, 3):
         act(hi("on", t, 608, 4), hi("zt", 0, 152))
     act(hi("on", 1, 512, 4), hi("s16", 0, 128), scale=-1.0 / 32)
-    act(hi("on", 0, 512, 4), hi("hh", 0, 128), scale=-0.5)
-    act(hi("on", 512, 608, 4), hi("one", 0, 24), scale=-0.5)
+    act(hi("on", 2, 512, 4), hi("hh", 0, 128), scale=-0.5)
+    act(hi("on", 514, 608, 4), hi("one", 0, 24), scale=-0.5)
 
     quant("erq", 0, 192, "ert", 0)
     quant("erq", 192, 192, "ert", 768)
     for b in range(4):
         mm(b, 384, "eq", 128 * b, "erq", 0)
-    ts(CORR, P15, 15.0, A_.is_lt, 512.0, A_.mult)
-    ts(XB10, P15, 10.0, A_.subtract, 0.0, A_.max)
-    ts(V("d16", 0, 128), V("s16", 0, 128), P15, A_.subtract)
     quant("uq", 0, 128, "urep", 0)
-    ts(V("sm1", 0, 128), V("d16", 0, 128), 0.0, A_.is_equal, -4096.0, A_.mult)
-    ts(V("sm2", 0, 128), V("d16", 0, 128), 1.0, A_.is_equal, 512.0, A_.mult)
-    for name in ("ao", "wtl", "f3"):
-        zero(name, 0, 512)
+    quant("onq", 0, 152, "on", 0)
+    for k in range(4):
+        ts(V("cf", 8 + k, 9 + k), P3, 4.0, A_.mult, float(own[k]), A_.add)
+    zero("lt", 0, 608)
+    iota(V("lt", 1, 512, 4), [[7, 2], [3, 2], [0, 32]], 0, 0)
+    iota(V("lt", 513, 608, 4), [[0, 24]], 1, 0)
+    sel(V("mask24a", 0, 24), V("one", 0, 24), [[0, 4], [-16, 6]], A_.is_ge, 0.0, 0, 1)
+    sel(V("mask24", 0, 24), V("mask24a", 0, 24), [[0, 4], [16, 6]], A_.is_ge, 0.0, 15, -1)
+    sel(V("mk", 0, 16), V("one", 0, 16), [[1, 4], [-1, 4]], A_.is_equal, 0.0, 0, 0)
+    for name in ("wtl", "a3"):
+        iota(V(name, 0, 512), [[0, 512]], 0, 0)
+    zero("ao", 0, 512)
+    act(V("mc", 0, 6), V("mcb", 0, 6), F_.Identity, bias=P15)
+    zero("vt", 768, 896)
+    zero("at", 384, 512)
+    zero("zw", 96, 128)
     at0 = [0, 96, 224, 320]
 
-    def score(c, bank, src):
-        act(lo("sa", c, c + 1), PS(bank, 0, 1, 1, 0, 96), F_.Identity, bias=2.0 ** -87, scale=2.0 ** 30)
-
-    def raised(o, c0, c):
-        act(lo(o, c0, c0 + 96), lo("tri", 0, 96), F_.Abs, bias=lo("sa", c, c + 1), scale=lo("sa", c, c + 1))
+    def score(c, bank):
+        act(lo("sa", c, c + 1), PS(bank, 0, 1, 1, 0, 96), F_.Abs, bias=TINY[:4] + (0, 96), scale=2.0 ** 30)
 
     def sizes(o, c0, n, bank):
-        act(lo(o, c0, c0 + n), PS(bank, 0, n, 1, 0, 96), F_.Abs, bias=V("cf", 15, 16, 1, 0, 96), scale=2.0 ** 30)
+        act(V(o, c0, c0 + n), PS(bank, 0, n), F_.Abs, bias=TINY, scale=2.0 ** 30)
+
+    def raised(q, o, c0, c):
+        if q == "a":
+            act(lo(o, c0, c0 + 96), lo("tri", 0, 96), F_.Identity, bias=lo("sa", c, c + 1), scale=lo("sa", c, c + 1))
+        else:
+            ts(lo(o, c0, c0 + 96), lo("tri", 0, 96), lo("sa", c, c + 1), A_.mult, lo("sa", c, c + 1), A_.add)
 
     RB, SB = (4, 7), (5, 6, 2, 3)
-    fill(V("cf", 15, 16), 2.0 ** -87)
-    for b in range(4):
-        for k in range(4):
-            tt(V("vt", 4 * at0[k] + b, 4 * at0[k] + 384, 4), PS(b, own[k], 384, 4), V("grt", 4 * own[k] + b, 1536, 16), A_.add)
     for h in range(2):
+        for b in range(4):
+            for k in (2 * h, 2 * h + 1):
+                tt(V("vt", 4 * at0[k] + b, 4 * at0[k] + 384, 4), PS(b, own[k], 384, 4), V("grt", 4 * own[k] + b, 1536, 16), A_.add)
         quant("qb", at0[2 * h], 192, "vt", 4 * at0[2 * h])
         mm(SB[2 * h], 128, "qb", at0[2 * h], "uq", 0)
         mm(SB[2 * h + 1], 128, "qb", at0[2 * h + 1], "uq", 0)
         mm(RB[h], 192, "uq", 0, "qb", at0[2 * h])
-    fill(hi("tt", 0, 512), 1.0)
-    for k in range(4):
-        ts(V("ofs", 3 * k, 3 * k + 1), XB10, 640.0 + 6 * k, A_.add)
-    tt(V("sm", 0, 128), V("sm1", 0, 128), V("sm2", 0, 128), A_.add)
-    quant("onq", 0, 152, "on", 0)
-    for h in range(2):
         for k in (2 * h, 2 * h + 1):
-            score(k, SB[k], None)
-        for k in (2 * h, 2 * h + 1):
-            raised("ss", 96 * k, k)
+            score(k, SB[k])
+        if h == 0:
+            for k in (0, 1):
+                raised("a", "ss", 96 * k, k)
         sizes("z", 192 * h, 192, RB[h])
     for k in range(4):
+        if k == 2:
+            quant("ahlq", 0, 128, "ahl", 0)
+            ts(lo("ao", 0, 512, 4), lo("s16", 0, 128), P15[:4] + (0, 96), A_.is_equal)
+            fill(hi("ao", 1, 512, 4), 1.0)
+            for k2 in (2, 3):
+                raised("v", "ss", 96 * k2, k2)
         tt(lo("tt", k, 384, 4), lo("z", 96 * k, 96 * k + 96), lo("ss", 96 * k, 96 * k + 96), A_.is_lt)
-        if k == 1:
-            for k2, x in ((1, 3), (2, 7), (3, 10)):
-                fill(hi("lt", 128 * k2 + 1, 128 * k2 + 128, 4), x / 32)
-            fill(hi("lt", 513, 608, 4), 1.0)
     quant("ttq", 0, 128, "tt", 0)
     mm(0, 152, "ttq", 0, "onq", 0)
-    quant("ahlq", 0, 128, "ahl", 0)
-    tt(lo("lt", 512, 608, 4), PS(0, 128, 152, 1, 0, 96), lo("mask24", 0, 24), A_.mult)
+    quant("aoq", 0, 128, "ao", 0)
+    ts(XB8, P15, 8.0, A_.subtract, 0.0, A_.max)
+    fill(V("ofd", 0, 32), 48)
     for t in range(2):
         ts(lo("lt", t, 512, 4), PS(0, 0, 128, 1, 0, 96), 0.0, A_.is_equal)
-    quant("qb", 512, 152, "lt", 0)
+    tt(lo("lt", 512, 608, 4), PS(0, 128, 152, 1, 0, 96), lo("mask24", 0, 24), A_.mult)
+    quant("qb", 512, 128, "lt", 0)
     mm(1, 128, "ahlq", 0, "qb", 512)
-    ts(XB8, P15, 8.0, A_.subtract, 0.0, A_.max)
+    quant("qb", 640, 128, "lt", 96)
+    ts(V("ofw", 0, 1), XB8, 288.0, A_.add)
     fill(V("fot", 384, 512), 0.0)
+    ts(V("cf", 4, 5), PK, 2.0, A_.is_ge, 32.0, A_.mult)
     scan("sc", 128, 1)
-    ts(V("ofs", 1, 12, 3), V("sc", 15, 128, 32), CORR, A_.subtract)
-    ts(V("ofs", 2, 12, 3), V("sc", 31, 128, 32), CORR, A_.subtract)
-    pick("send", 16, "qb", 0, 664, "ofs", 0, 8)
-    pick("send", 144, "qb", 0, 664, "ofs", 8, 12)
+    ts(V("ofs", 1, 9, 3), V("sc", 15, 96, 32), CORR, A_.subtract)
+    ts(V("ofs", 2, 9, 3), V("sc", 31, 96, 32), CORR, A_.subtract)
+    ts(V("ofo3", 1, 3), V("sc", 111, 128, 16), CORR, A_.subtract)
+    pick("send", 16, "qb", 0, 768, "ofs", 0, 9)
 
     eng = topo.engines(core, T.cores[own[0]])
     for k in range(3):
@@ -313,38 +350,33 @@ def rank_program(g, core, T, topo):
     send("send", [26 + 48 * k for k in range(3)], ["land0", "land1", "land2"], [10] * 3, 38, ["arr0", "arr1", "arr2"])
     for x in range(3):
         note(("arr%d" % x, arrive[x], {}), "far", [V("land%dc" % x, 10, 48), V("land%ds" % x, 10, 48)], [])
+    pick("send", 160, "qb", 0, 768, "ofo3", 0, 3)
 
     quant("pw", 128, 128, "fot", 0)
     for b in range(4):
         mm(b, 416, "eq", 128 * b, "qb", 0)
     for b in range(4):
         mm(4 + b, 128, "eq", 128 * b, "pw", 128, True, False)
-    ts(lo("ao", 0, 512, 4), lo("s16", 0, 128), P15[:4] + (0, 96), A_.is_equal)
-    fill(hi("ao", 1, 512, 4), 1.0)
-    fill(V("ofd", 0, 32), 48)
-    quant("send", 208, 128, "zt", 0)
-    quant("aoq", 0, 128, "ao", 0)
-    for x in range(3):
-        quant("land%d" % x, 48, 128, "zt", 0)
-    fill(V("vt", 768, 896), 0.0)
-    fill(V("at", 384, 512), 0.0)
-    ts(V("ofw", 0, 1), XB8, 288.0, A_.add)
     for b in range(4):
         tt(V("left", b, 1664, 4), V("vt", b, 1664, 4), PS(b, 0, 416), A_.subtract)
-    iota(V("mcb", 0, 6), [[16, 6]], 0, 0)
-    iota(V("pos", 0, 24), [[4, 24]], 0, 0)
-    sel(V("mk", 0, 16), V("one", 0, 16), [[1, 4], [-1, 4]], A_.is_equal, 0.0, 0, 0)
+    mm(0, 128, "pw", 128, "uq", 0)
+    mm(1, 128, "uq", 0, "pw", 128)
     sel(lo("on", 608, 992), lo("one", 0, 384), [[0, 24], [1, 4], [-1, 4]], A_.is_equal, 0.0, 0, 0)
     sel(V("thr3a", 0, 96), V("zt", 0, 96), [[-4, 24], [0, 4]], A_.is_ge, -1000.0, 0, 1)
     sel(V("thr6a", 0, 6), V("zt", 0, 6), [[-16, 6]], A_.is_ge, -1000.0, 0, 1)
     sel(V("thr3", 0, 96), V("thr3a", 0, 96), [[4, 24], [0, 4]], A_.is_ge, -1000.0, 3, -1)
     sel(V("thr6", 0, 6), V("thr6a", 0, 6), [[16, 6]], A_.is_ge, -1000.0, 15, -1)
-    act(V("mc", 0, 6), V("mcb", 0, 6), F_.Identity, bias=P15)
+    for name in ("mh", "ml", "f3", "f5"):
+        iota(V(name, 0, 512), [[0, 512]], 0, 0)
     act(hi("wtl", 128, 160), hi("one", 0, 32), scale=rk / 32.0)
-    for name in ("mh", "ml", "a3"):
-        zero(name, 0, 512)
-    act(hi("ml", 0, 16), hi("mk", 0, 16))
-    quant("pb", 0, 128, "zt", 0)
+    act(lo("on", 992, 1120), lo("zt", 0, 128))
+    for t in (0, 2, 3):
+        act(hi("on", 608 + t, 1120, 4), hi("zt", 0, 128))
+    act(hi("on", 993, 1120, 4), hi("zt", 0, 32))
+    act(hi("on", 609, 992, 4), hi("one", 0, 96), scale=-1.0)
+    SF, UN, NM, BFT = [V("cg", c, c + 1) for c in range(4)]
+    act(SF, PS(0, 0, 1), F_.Identity, scale=2.0 ** 23)
+    sizes("zw", 128, 96, 1)
 
     def place(s):
         return ("send", 160) if s == rk else ("land%d" % ((s - rk - 1) % N), 0)
@@ -352,99 +384,105 @@ def rank_program(g, core, T, topo):
     def offsets(s):
         mm(s, 128, "aoq", 0, place(s)[0], place(s)[1] + 10)
 
-    def add(s):
+    def dense(s):
+        w, c = place(s)
+        pick("den", 128 * s, w, c, c + 138, "ofd", 8 * s, 8 * s + 8)
+
+    far = [s for s in range(N) if s != rk]
+    offsets(rk)
+    copy(V("ofd", 8 * rk, 8 * rk + 6), PS(rk, 0, 6))
+    copy(V("mn", 0, 6), PS(rk, 0, 6))
+    dense(rk)
+    for s in far:
+        offsets(s)
+    for s in range(N):
+        if s == far[0]:
+            for x in far:
+                copy(V("ofd", 8 * x, 8 * x + 6), PS(x, 0, 6))
+            dense(far[0])
+            for i in (0, 1):
+                tt(V("mn", 6 * i + 6, 6 * i + 12), PS(far[i], 0, 6), V("mn", 6 * i, 6 * i + 6), A_.min)
+        elif s == far[1]:
+            dense(s)
+            tt(V("mn", 18, 24), PS(far[2], 0, 6), V("mn", 12, 18), A_.min)
+        elif s == far[2]:
+            dense(s)
         for b in range(4):
             mm(4 + b, 128, "eq", 128 * b, "den", 128 * s, False, s == N - 1)
-
-    offsets(0)
-    for s in range(4):
-        if s < 3:
-            offsets(s + 1)
-        copy(V("ofd", 8 * s, 8 * s + 6), PS(s, 0, 6))
-        if s == 0:
-            copy(V("mn", 0, 6), PS(0, 0, 6))
-        else:
-            tt(V("mn", 6 * s, 6 * s + 6), PS(s, 0, 6), V("mn", 6 * s - 6, 6 * s), A_.min)
-        w, c = place(s)
-        pick("den", 128 * s, w, c, c + 176, "ofd", 8 * s, 8 * s + 8)
-        add(s)
     ts(V("pu", 0, 6), V("mn", 18, 24), 48.0, A_.is_ge, 128.0, A_.mult)
-    ts(V("cf", 4, 5), PK, 2.0, A_.is_ge, 32.0, A_.mult)
-    tt(V("pl", 0, 6), V("pu", 0, 6), V("mc", 0, 6), A_.add)
-    ts(V("cf", 6, 7), P8, 4.0, A_.mult)
-    copy(V("ofp", 0, 6), V("pl", 0, 6))
-    for b in range(4):
-        o, i = V("at", b, 384, 4), PS(4 + b, 0, 96)
-        if b % 2:
-            act(o, i)
-        else:
-            copy(o, i)
-    quant("pw", 0, 128, "at", 0)
-    pick("pb", 0, "pw", 0, 256, "ofp", 0, 6)
-    mm(1, 128, "pb", 0, "uq", 0)
-    mm(0, 128, "uq", 0, "pb", 0)
-    score(4, 1, None)
-    raised("ss2", 0, 4)
-    sizes("z2", 0, 96, 0)
     ts(V("cf", 5, 6), PK, 96.0, A_.mult, V("cf", 4, 5), A_.add)
+    ts(V("cf", 6, 7), P8, 4.0, A_.mult)
+    tt(V("pl", 0, 6), V("pu", 0, 6), V("mc", 0, 6), A_.add)
+    tt(V("pm", 0, 6), V("pu", 0, 6), V("mask24", 0, 6), A_.mult)
     ts(V("cf", 7, 8), P7, 4.0, A_.mult)
-    for k in range(4):
-        ts(V("cf", 8 + k, 9 + k), P3, 4.0, A_.mult, float(own[k]), A_.add)
-    ts(V("posc", 0, 24), V("pos", 0, 24), V("cf", 5, 6), A_.add, P42, A_.add)
+    copy(V("ofp", 0, 6), V("pl", 0, 6))
+    run("v", lambda: g.vector.tensor_reduce(ap(UN), ap(V("pm", 0, 6)), AxisListType.X, A_.add), [UN], [V("pm", 0, 6)])
+    for b in range(4):
+        copy(V("at", b, 384, 4), PS(4 + b, 0, 96))
+        if b == 1:
+            ts(NM, UN, 0.0, A_.is_equal, 2.0 ** 30, A_.mult)
+            ts(BFT, UN, SF, A_.mult, 2.0 ** -87, A_.add)
+    quant("pw", 0, 128, "at", 0)
+    pick_codes("pb", 0, "pw", 0, 256, "ofp", 0, 6)
+    mm(1, 128, "pw", 0, "uq", 0)
+    mm(0, 128, "uq", 0, "pw", 0)
+    act(V("sa", 4, 5), PS(1, 0, 1), F_.Abs, bias=BFT, scale=NM)
+    sizes("zw", 0, 96, 0)
+    pick_scales("pb", 0, "pw", 0, 256, "ofp", 0, 6)
+    act(lo("mh", 0, 16), lo("mk", 0, 16), scale=V("cf", 6, 7, 1, 0, 96))
+    act(lo("ml", 0, 16), lo("mk", 0, 16), scale=V("cf", 7, 8, 1, 0, 96))
+    act(hi("ml", 0, 16), hi("mk", 0, 16))
+    zero("left2", 384, 512)
     for k in range(4):
         ts(lo("a3", k, 512, 4), lo("s16", 0, 128), V("cf", 8 + k, 9 + k, 1, 0, 96), A_.is_equal, 768.0, A_.mult)
-    tt(lo("tt", 0, 384, 4), lo("z2", 0, 96), lo("ss2", 0, 96), A_.is_lt)
+    ts(V("ss2", 0, 96), V("tri", 0, 96), V("sa", 4, 5), A_.mult, V("sa", 4, 5), A_.add)
+    tt(V("tt", 0, 384, 4), V("zw", 0, 224), V("ss2", 0, 96), A_.is_lt, V("ofp", 0, 6))
+    quant("onq", 152, 128, "on", 608)
     quant("ttr", 0, 128, "tt", 0)
     mm(2, 128, "ttr", 0, "onq", 0)
     quant("a3q", 0, 128, "a3", 0)
-    ts(lo("mh", 0, 16), lo("mk", 0, 16), V("cf", 6, 7, 1, 0, 96), A_.mult)
-    ts(lo("ml", 0, 16), lo("mk", 0, 16), V("cf", 7, 8, 1, 0, 96), A_.mult)
+    quant("mhq", 0, 128, "mh", 0)
     for t in range(2):
         ts(lo("wtl", t, 128, 4), PS(2, 0, 32, 1, 0, 96), 0.0, A_.is_equal)
+    ts(V("posc", 0, 24), V("pos", 0, 24), V("cf", 5, 6), A_.add, P42, A_.add)
+    quant("lq", 0, 128, "wtl", 0)
+    mm(3, 128, "ahlq", 0, "lq", 0)
     ts(lo("wtl", 128, 160), PS(2, 0, 32, 1, 0, 96), 0.0, A_.is_equal)
+    quant("mlq", 0, 128, "ml", 0)
     quant("pb", 256, 128, "wtl", 0)
-    mm(3, 128, "ahlq", 0, "pb", 256)
-    quant("wq", 0, 128, "wt", 0)
     scan("sc2", 32, 3)
+    for b in range(4):
+        mm(4 + b, 128, "eq", 128 * b, "pb", 0)
+    mm(0, 128, "ttq", 0, "onq", 152)
+    mm(2, 128, "ttr", 0, "onq", 152)
     ts(V("ofw", 1, 3), V("sc2", 15, 32, 16), CORR, A_.subtract)
     pick("ws", 0, "pb", 0, 384, "ofw", 0, 3)
     send("ws", [8] * 3, ["wl", "wl", "wl"], [48 + 40 * x for x in range(3)], 40, ["arw0", "arw1", "arw2"])
     for x in range(3):
         c0 = 48 + 40 * x
         note(("arw%d" % x, arrive[x], {}), "far", [V("wlc", c0, c0 + 40), V("wls", c0, c0 + 40)], [])
-    pick("wl", 0, "pb", 0, 384, "ofw", 0, 3)
 
-    act(lo("on", 992, 1120), lo("zt", 0, 128))
-    for t in (1, 2, 3):
-        act(hi("on", 608 + t, 1120, 4), hi("zt", 0, 128))
-    act(hi("on", 992, 1120, 4), hi("zt", 0, 32))
-    act(hi("on", 608, 992, 4), hi("one", 0, 96), scale=-1.0)
-    zero("left2", 384, 512)
-    zero("f5", 0, 512)
-    for b in range(4):
-        mm(4 + b, 128, "eq", 128 * b, "pb", 0)
-    quant("qb", 768, 416, "left", 0)
-    quant("mhq", 0, 128, "mh", 0)
-    quant("mlq", 0, 128, "ml", 0)
-    quant("onq", 152, 128, "on", 608)
-    mm(0, 128, "ttq", 0, "onq", 152)
-    mm(2, 128, "ttr", 0, "onq", 152)
-    for b in range(4):
-        tt(V("left2", b, 384, 4), V("at", b, 384, 4), PS(4 + b, 0, 96), A_.subtract)
     tt(lo("f3", 0, 96), PS(0, 0, 96, 1, 0, 96), lo("thr3", 0, 96), A_.is_lt)
     tt(lo("f5", 0, 24, 4), PS(2, 0, 24, 4, 0, 96), lo("thr6", 0, 6), A_.is_lt)
+    pick("wl", 0, "pb", 0, 384, "ofw", 0, 3)
     quant("f3q", 0, 128, "f3", 0)
     mm(1, 128, "a3q", 0, "f3q", 0)
     quant("f5q", 0, 128, "f5", 0)
     mm(3, 128, "aoq", 0, "f5q", 0)
-    quant("pb", 128, 128, "left2", 0)
+    quant("qb", 768, 416, "left", 0)
     tt(V("et", 0, 24), PS(1, 0, 24), V("posc", 0, 24), A_.add)
     ts(V("et2", 0, 6), PS(3, 0, 6), 128.0, A_.mult)
+    for b in (0, 1):
+        tt(V("left2", b, 384, 4), V("at", b, 384, 4), PS(4 + b, 0, 96), A_.subtract)
     copy(V("ofe", 0, 24), V("et", 0, 24))
     tt(V("et2", 6, 12), V("et2", 0, 6), V("mc", 0, 6), A_.add)
+    for b in (2, 3):
+        tt(V("left2", b, 384, 4), V("at", b, 384, 4), PS(4 + b, 0, 96), A_.subtract)
     pick("oe", 0, "qb", 0, 1184, "ofe", 0, 24)
     dma("s", None, V("oec", 0, 384), oap=T.oc[:, 0:1536], iap=T.oec[:, 0:384].bitcast(dt.uint8))
+    quant("pb", 128, 128, "left2", 0)
     copy(V("ofo", 0, 6), V("et2", 6, 12))
+    quant("wq", 0, 128, "wt", 0)
     pick("oe", 384, "pb", 0, 256, "ofo", 0, 6)
     dma("s", None, V("oec", 384, 480), oap=T.oc[:, 1536:1920], iap=T.oec[:, 384:480].bitcast(dt.uint8))
     for k in range(4):

@@ -8,24 +8,23 @@ STEP = 1.25 * 2.0 ** -24
 SCRATCH = {"ps": ("psum", [128, 4096], F32)}
 for _n, _w, _d in (
         ("ert", 1536, BF), ("grt", 1536, BF), ("fot", 512, BF), ("wt", 512, BF), ("uc", 4, BF), ("ucf", 4, F32),
-        ("one", 512, BF), ("cst", 96, BF), ("zt", 608, BF), ("ew", 520, BF), ("urep", 512, BF), ("tri", 96, BF), ("s16", 128, BF),
+        ("one", 512, BF), ("cst", 96, BF), ("zt", 512, BF), ("ew", 520, BF), ("urep", 512, BF), ("tri", 96, BF), ("s16", 128, BF),
         ("hh", 128, BF), ("mask24", 24, BF), ("mask24a", 24, BF), ("on", 1120, BF), ("tt", 512, BF), ("lt", 608, BF), ("ahl", 512, BF),
-        ("ao", 512, BF), ("a3", 512, BF), ("f3", 512, BF), ("f5", 512, BF), ("wtl", 512, BF), ("mk", 16, BF),
-        ("mh", 512, BF), ("ml", 512, BF), ("vt", 1664, BF), ("left", 1664, BF), ("at", 512, BF), ("left2", 512, BF),
+        ("ao", 512, BF), ("a3", 512, BF), ("f35", 608, BF), ("wtl", 512, BF), ("mk", 16, BF),
+        ("hm", 528, BF), ("vt", 1536, BF), ("left", 1536, BF), ("at", 512, BF), ("left2", 512, BF),
         ("d16", 128, BF), ("sm1", 128, BF), ("sm2", 128, BF), ("sm", 128, BF), ("thr3", 96, BF), ("thr3a", 96, BF), ("thr6", 6, BF), ("thr6a", 6, BF),
         ("icol", 8, I32), ("ci", 8, F32), ("cf", 16, F32), ("cg", 8, F32), ("k6", 4, F32), ("pos", 24, F32), ("posc", 24, F32), ("mcb", 6, F32), ("mc", 6, F32),
         ("sa", 8, F32), ("z", 384, F32), ("ss", 384, F32), ("zw", 224, F32), ("ss2", 96, F32),
         ("sc", 128, F32), ("sc2", 32, F32), ("mn", 24, F32), ("pu", 6, F32), ("pm", 6, F32), ("pl", 6, F32), ("et", 24, F32), ("et2", 12, F32),
-        ("ysb", 128, F32), ("nbs", 4, F32),
+        ("ysb", 128, F32), ("nbs", 8, F32),
         ("ofs", 10, U16), ("ofo3", 4, U16), ("ofd", 32, U16), ("ofp", 6, U16), ("ofw", 4, U16), ("ofe", 24, U16), ("ofo", 6, U16)):
     SCRATCH[_n] = ("sbuf", [128, _w], _d)
-for _n, _w in (("erq", 384), ("eq", 512), ("uq", 128), ("zq", 128), ("onq", 280), ("ttq", 128), ("ttr", 128), ("ahlq", 128), ("aoq", 128),
-               ("a3q", 128), ("f3q", 128), ("f5q", 128), ("mhq", 128), ("mlq", 128), ("wq", 128), ("lq", 128), ("qb", 1184), ("send", 336),
-               ("land0", 176), ("land1", 176), ("land2", 176), ("den", 512), ("pw", 256), ("pb", 384), ("ws", 48),
-               ("wl", 168), ("oe", 480)):
+for _n, _w in (("erq", 384), ("eq", 512), ("uq", 128), ("onq", 280), ("ttq", 128), ("ttr", 128), ("ahlq", 128), ("aoq", 128),
+               ("a3q", 128), ("f3q", 128), ("f5q", 128), ("hmq", 132), ("wq", 128), ("lq", 128), ("qb", 1152), ("send", 336),
+               ("land0", 176), ("land1", 176), ("land2", 176), ("den", 416), ("pw", 256), ("pb", 384), ("wl", 128), ("oe", 480)):
     SCRATCH[_n + "c"] = ("sbuf", [128, _w], CODE)
     SCRATCH[_n + "s"] = ("sbuf", [128, _w], PLANE)
-SEMAPHORES = ["qv", "qa", "qt", "qg", "ls", "arr0", "arr1", "arr2", "arw0", "arw1", "arw2"] + ["d%d" % _i for _i in range(32)]
+SEMAPHORES = ["qv", "qa", "qt", "qg", "ls", "arr0", "arr1", "arr2", "arw0", "arw1", "arw2"] + ["d%d" % _i for _i in range(40)]
 
 
 def rank_program(g, core, T, topo):
@@ -177,26 +176,26 @@ def rank_program(g, core, T, topo):
         return V(name, c0, c1, step, 96, 128)
 
     dma("s", V("ert", 0, 768), None, iap=T.er[:, 0:768])
+    dma("a", V("uc", 0, 4), None, iap=T.u[:, 0:4])
     dma("a", V("ert", 768, 1536), None, iap=T.er[:, 768:1536])
     dma("s", V("grt", 0, 1536), None, iap=T.gr[:, :])
-    dma("a", V("uc", 0, 4), None, iap=T.u[:, 0:4])
     wait("s", [dma_tok[2][1]])
     dma("s", V("fot", 0, 384), None, iap=T.fo[:, :])
     dma("s", V("wt", 0, 512), None, iap=T.w[:, :])
 
     iota(V("icol", 0, 1), [[0, 1]], 0, 1, small=False)
-    iota(V("s16", 0, 128), [[0, 8], [1, 16]], 0, 0)
-    fill(V("one", 0, 512), 1.0)
+    iota(V("icol", 5, 6), [[0, 1]], N - 1 - rk, 1, small=False)
+    fill(V("one", 0, 128), 1.0)
     fill(V("ew", 0, 520), 0.0)
     sel(V("ew", 3, 515, 4), V("one", 0, 128), [[-1, 128]], A_.is_equal, 0.0, 0, 1)
-    fill(V("zt", 0, 608), 0.0)
+    iota(V("s16", 0, 128), [[0, 8], [1, 16]], 0, 0)
+    fill(V("zt", 0, 512), 0.0)
+    act(V("one", 128, 512), V("zt", 0, 384), F_.Identity, bias=1.0)
     for c, x in ((1, 15), (2, 7), (3, 3)):
         ts(V("icol", c, c + 1), V("icol", 0, 1), x, A_.bitwise_and)
-    ts(V("icol", 5, 6), V("icol", 0, 1), N - 1 - rk, A_.add)
     ts(V("icol", 4, 5), V("icol", 0, 1), 15, A_.bitwise_and, 2, A_.logical_shift_right)
-    fill(V("cst", 0, 96), STEP)
     ts(V("icol", 6, 7), V("icol", 5, 6), 3, A_.bitwise_and)
-    quant("qb", 192, 128, "zt", 0)
+    fill(V("cst", 0, 96), STEP)
     P0, P15, P7, P3, P42, PK = [V("ci", c, c + 1) for c in (0, 1, 2, 3, 4, 6)]
     P8, CORR, XB8, TINY = [V("cf", c, c + 1) for c in (0, 1, 3, 15)]
     copy(V("ci", 0, 7), V("icol", 0, 7))
@@ -207,120 +206,111 @@ def rank_program(g, core, T, topo):
         quant("eq", 128 * b, 128, "ew", 3 - b)
         if b == 0:
             tt(P8, P0, P7, A_.subtract)
-            ts(V("d16", 0, 128), V("s16", 0, 128), P15, A_.subtract)
-            ts(CORR, P15, 15.0, A_.is_lt, 512.0, A_.mult)
-        if b == 1:
-            ts(V("sm1", 0, 128), V("d16", 0, 128), 0.0, A_.is_equal, -4096.0, A_.mult)
-            ts(V("sm2", 0, 128), V("d16", 0, 128), 1.0, A_.is_equal, 512.0, A_.mult)
-    quant("qb", 320, 128, "zt", 0)
-    quant("zq", 0, 128, "zt", 0)
-    for name, c, n in (("land0", 48, 90), ("land1", 48, 90), ("land2", 48, 90), ("send", 208, 90), ("pb", 96, 32)):
-        o, i = V(name + "c", c, c + n), V("zqc", 0, n)
+            fill(TINY, 2.0 ** -87)
+    quant("erq", 0, 192, "ert", 0)
+    quant("erq", 192, 192, "ert", 768)
+    quant("qb", 384, 128, "zt", 0)
+    for name, c, n in (("land0", 48, 90), ("land1", 48, 90), ("land2", 48, 90), ("send", 208, 90), ("pb", 96, 32), ("den", 384, 32), ("wl", 120, 8)):
+        o, i = V(name + "c", c, c + n), V("qbc", 384, 384 + n)
         dma("s", o, i, ap(o).bitcast(dt.uint8), ap(i).bitcast(dt.uint8))
-        dma("s", V(name + "s", c, c + n), V("zqs", 0, n))
-    fill(hi("tt", 0, 512), 1.0)
-    fill(TINY, 2.0 ** -87)
-    ts(V("ofs", 0, 9, 3), V("k6", 0, 3), P15, A_.add)
-    ts(V("ofo3", 0, 1), V("k6", 3, 4), P15, A_.add)
-    tt(V("sm", 0, 128), V("sm1", 0, 128), V("sm2", 0, 128), A_.add)
-
+        dma("s", V(name + "s", c, c + n), V("qbs", 384, 384 + n))
     sel(lo("on", 0, 512), lo("one", 0, 512), [[1, 4], [0, 32], [-1, 4]], A_.is_equal, 0.0, 0, 0)
     sel(lo("on", 512, 608), lo("one", 0, 96), [[1, 4], [0, 6], [-1, 4]], A_.is_equal, 0.0, 0, 0)
-    iota(V("pos", 0, 24), [[4, 24]], 0, 0)
+    iota(V("pos", 0, 24), [[4, 24]], 192, 0)
     iota(V("mcb", 0, 6), [[16, 6]], 0, 0)
 
-    act(lo("tt", 0, 512), lo("zt", 0, 512))
+    act(hi("on", 1, 512, 4), hi("s16", 0, 128), scale=-1.0 / 32)
+    act(V("ucf", 0, 4), V("uc", 0, 4))
+    for t in range(4):
+        act(V("urep", t, 512, 4), V("one", 0, 128), scale=V("ucf", t, t + 1))
+    act(hi("on", 2, 512, 4), hi("hh", 0, 128), scale=-0.5)
+    act(hi("on", 513, 608, 4), hi("zt", 0, 24))
+    act(hi("on", 514, 608, 4), hi("one", 0, 24), scale=-0.5)
+    for t in (0, 3):
+        act(hi("on", t, 608, 4), hi("zt", 0, 152))
     zero("ahl", 0, 512)
     act(lo("ahl", 0, 512, 4), lo("one", 0, 128), scale=P8[:4] + (0, 96))
     act(lo("ahl", 1, 512, 4), lo("one", 0, 128), scale=P7[:4] + (0, 96))
     act(hi("ahl", 1, 512, 4), hi("one", 0, 128))
-    act(V("ucf", 0, 4), V("uc", 0, 4))
-    for t in range(4):
-        act(V("urep", t, 512, 4), V("one", 0, 128), scale=V("ucf", t, t + 1))
-    act(hi("on", 513, 608, 4), hi("zt", 0, 24))
-    for t in (0, 3):
-        act(hi("on", t, 608, 4), hi("zt", 0, 152))
-    act(hi("on", 1, 512, 4), hi("s16", 0, 128), scale=-1.0 / 32)
-    act(hi("on", 2, 512, 4), hi("hh", 0, 128), scale=-0.5)
-    act(hi("on", 514, 608, 4), hi("one", 0, 24), scale=-0.5)
+    act(lo("tt", 384, 512), lo("zt", 0, 128))
+    zero("lt", 0, 512)
+    zero("lt", 512, 608)
 
-    quant("erq", 0, 192, "ert", 0)
-    quant("erq", 192, 192, "ert", 768)
     for b in range(4):
         mm(b, 384, "eq", 128 * b, "erq", 0)
     quant("uq", 0, 128, "urep", 0)
-    quant("onq", 0, 152, "on", 0)
-    for k in range(4):
-        ts(V("cf", 8 + k, 9 + k), P3, 4.0, A_.mult, float(own[k]), A_.add)
-    zero("lt", 0, 608)
-    iota(V("lt", 1, 512, 4), [[7, 2], [3, 2], [0, 32]], 0, 0)
+    fill(hi("tt", 0, 512), 1.0)
+    at0 = [192, 288, 0, 96]
+    for b in range(4):
+        for k in range(4):
+            tt(V("vt", 4 * at0[k] + b, 4 * at0[k] + 384, 4), PS(b, own[k], 384, 4), V("grt", 4 * own[k] + b, 1536, 16), A_.add)
+    quant("qb", 192, 192, "vt", 768)
+    quant("qb", 0, 192, "vt", 0)
+    iota(V("lt", 1, 512, 4), [[-6, 2], [3, 2], [0, 32]], 6, 0)
     iota(V("lt", 513, 608, 4), [[0, 24]], 1, 0)
     sel(V("mask24a", 0, 24), V("one", 0, 24), [[0, 4], [-16, 6]], A_.is_ge, 0.0, 0, 1)
     sel(V("mask24", 0, 24), V("mask24a", 0, 24), [[0, 4], [16, 6]], A_.is_ge, 0.0, 15, -1)
     sel(V("mk", 0, 16), V("one", 0, 16), [[1, 4], [-1, 4]], A_.is_equal, 0.0, 0, 0)
-    for name in ("wtl", "a3"):
-        iota(V(name, 0, 512), [[0, 512]], 0, 0)
-    zero("ao", 0, 512)
-    act(V("mc", 0, 6), V("mcb", 0, 6), F_.Identity, bias=P15)
-    zero("vt", 768, 896)
-    zero("at", 384, 512)
-    zero("zw", 96, 128)
-    at0 = [0, 96, 224, 320]
+    iota(V("wtl", 0, 512), [[0, 512]], 0, 0)
+    iota(V("hm", 0, 528), [[0, 528]], 0, 0)
 
     def score(c, bank):
         act(lo("sa", c, c + 1), PS(bank, 0, 1, 1, 0, 96), F_.Abs, bias=TINY[:4] + (0, 96), scale=2.0 ** 30)
 
-    def sizes(o, c0, n, bank):
-        act(V(o, c0, c0 + n), PS(bank, 0, n), F_.Abs, bias=TINY, scale=2.0 ** 30)
+    def sizes(o, c0, n, bank, b0=0):
+        act(V(o, c0, c0 + n), PS(bank, b0, b0 + n), F_.Abs, bias=TINY, scale=2.0 ** 30)
 
-    def raised(q, o, c0, c):
-        if q == "a":
-            act(lo(o, c0, c0 + 96), lo("tri", 0, 96), F_.Identity, bias=lo("sa", c, c + 1), scale=lo("sa", c, c + 1))
-        else:
-            ts(lo(o, c0, c0 + 96), lo("tri", 0, 96), lo("sa", c, c + 1), A_.mult, lo("sa", c, c + 1), A_.add)
+    def raised(o, c0, c):
+        ts(lo(o, c0, c0 + 96), lo("tri", 0, 96), lo("sa", c, c + 1), A_.mult, lo("sa", c, c + 1), A_.add)
 
     RB, SB = (4, 7), (5, 6, 2, 3)
     for h in range(2):
-        for b in range(4):
-            for k in (2 * h, 2 * h + 1):
-                tt(V("vt", 4 * at0[k] + b, 4 * at0[k] + 384, 4), PS(b, own[k], 384, 4), V("grt", 4 * own[k] + b, 1536, 16), A_.add)
-        quant("qb", at0[2 * h], 192, "vt", 4 * at0[2 * h])
         mm(SB[2 * h], 128, "qb", at0[2 * h], "uq", 0)
         mm(SB[2 * h + 1], 128, "qb", at0[2 * h + 1], "uq", 0)
         mm(RB[h], 192, "uq", 0, "qb", at0[2 * h])
+    quant("onq", 0, 152, "on", 0)
+    quant("ahlq", 0, 128, "ahl", 0)
+    for h in range(2):
         for k in (2 * h, 2 * h + 1):
             score(k, SB[k])
+        for k in (0, 1):
+            sizes("z", 192 * h + 96 * k, 96, RB[h], 96 * k)
+    for h in range(2):
+        for k in (2 * h, 2 * h + 1):
+            raised("ss", 96 * k, k)
         if h == 0:
-            for k in (0, 1):
-                raised("a", "ss", 96 * k, k)
-        sizes("z", 192 * h, 192, RB[h])
-    for k in range(4):
-        if k == 2:
-            quant("ahlq", 0, 128, "ahl", 0)
-            ts(lo("ao", 0, 512, 4), lo("s16", 0, 128), P15[:4] + (0, 96), A_.is_equal)
-            fill(hi("ao", 1, 512, 4), 1.0)
-            for k2 in (2, 3):
-                raised("v", "ss", 96 * k2, k2)
-        tt(lo("tt", k, 384, 4), lo("z", 96 * k, 96 * k + 96), lo("ss", 96 * k, 96 * k + 96), A_.is_lt)
+            ts(V("d16", 0, 128), V("s16", 0, 128), P15, A_.subtract)
+        for k in (2 * h, 2 * h + 1):
+            tt(lo("tt", k, 384, 4), lo("z", 96 * k, 96 * k + 96), lo("ss", 96 * k, 96 * k + 96), A_.is_lt)
+    ts(CORR, P15, 15.0, A_.is_lt, 512.0, A_.mult)
     quant("ttq", 0, 128, "tt", 0)
     mm(0, 152, "ttq", 0, "onq", 0)
-    quant("aoq", 0, 128, "ao", 0)
-    ts(XB8, P15, 8.0, A_.subtract, 0.0, A_.max)
-    fill(V("ofd", 0, 32), 48)
+    ts(V("ofs", 0, 9, 3), V("k6", 0, 3), P15, A_.add)
+    ts(V("sm1", 0, 128), V("d16", 0, 128), 0.0, A_.is_equal, -4096.0, A_.mult)
+    ts(V("sm2", 0, 128), V("d16", 0, 128), 1.0, A_.is_equal, 512.0, A_.mult)
+    act(XB8, P15, F_.Relu, bias=-8.0)
+    for k in range(4):
+        act(V("cf", 8 + k, 9 + k), P3, F_.Identity, bias=float(own[k]), scale=4.0)
+    act(V("mc", 0, 6), V("mcb", 0, 6), F_.Identity, bias=P15)
+    zero("ao", 0, 512)
+    act(hi("ao", 1, 512, 4), hi("one", 0, 128))
+    zero("at", 384, 512)
+    zero("zw", 96, 128)
+    zero("fot", 384, 512)
     for t in range(2):
         ts(lo("lt", t, 512, 4), PS(0, 0, 128, 1, 0, 96), 0.0, A_.is_equal)
-    tt(lo("lt", 512, 608, 4), PS(0, 128, 152, 1, 0, 96), lo("mask24", 0, 24), A_.mult)
+    ts(V("ofo3", 0, 1), V("k6", 3, 4), P15, A_.add)
     quant("qb", 512, 128, "lt", 0)
     mm(1, 128, "ahlq", 0, "qb", 512)
+    tt(lo("lt", 512, 608, 4), PS(0, 128, 152, 1, 0, 96), lo("mask24", 0, 24), A_.mult)
+    tt(V("sm", 0, 128), V("sm1", 0, 128), V("sm2", 0, 128), A_.add)
     quant("qb", 640, 128, "lt", 96)
-    ts(V("ofw", 0, 1), XB8, 288.0, A_.add)
-    fill(V("fot", 384, 512), 0.0)
-    ts(V("cf", 4, 5), PK, 2.0, A_.is_ge, 32.0, A_.mult)
     scan("sc", 128, 1)
+    ts(V("cf", 4, 5), PK, 2.0, A_.is_ge, -384.0, A_.mult)
     ts(V("ofs", 1, 9, 3), V("sc", 15, 96, 32), CORR, A_.subtract)
     ts(V("ofs", 2, 9, 3), V("sc", 31, 96, 32), CORR, A_.subtract)
-    ts(V("ofo3", 1, 3), V("sc", 111, 128, 16), CORR, A_.subtract)
     pick("send", 16, "qb", 0, 768, "ofs", 0, 9)
+    ts(V("ofo3", 1, 3), V("sc", 111, 128, 16), CORR, A_.subtract)
 
     eng = topo.engines(core, T.cores[own[0]])
     for k in range(3):
@@ -350,24 +340,43 @@ def rank_program(g, core, T, topo):
     send("send", [26 + 48 * k for k in range(3)], ["land0", "land1", "land2"], [10] * 3, 38, ["arr0", "arr1", "arr2"])
     for x in range(3):
         note(("arr%d" % x, arrive[x], {}), "far", [V("land%dc" % x, 10, 48), V("land%ds" % x, 10, 48)], [])
-    pick("send", 160, "qb", 0, 768, "ofo3", 0, 3)
 
     quant("pw", 128, 128, "fot", 0)
+    ts(lo("ao", 0, 512, 4), lo("s16", 0, 128), P15[:4] + (0, 96), A_.is_equal)
+    pick("send", 160, "qb", 0, 768, "ofo3", 0, 3)
+    quant("aoq", 0, 128, "ao", 0)
+
+    def place(s):
+        return ("send", 160) if s == rk else ("land%d" % ((s - rk - 1) % N), 0)
+
+    def offsets(s, bank):
+        mm(bank, 128, "aoq", 0, place(s)[0], place(s)[1] + 10)
+
+    def dense(s):
+        w, c = place(s)
+        pick("den", 96 * (3 - s), w, c, c + 138, "ofd", 8 * s, 8 * s + 6)
+
     for b in range(4):
-        mm(b, 416, "eq", 128 * b, "qb", 0)
+        mm(b, 384, "eq", 128 * b, "qb", 0)
     for b in range(4):
         mm(4 + b, 128, "eq", 128 * b, "pw", 128, True, False)
-    for b in range(4):
-        tt(V("left", b, 1664, 4), V("vt", b, 1664, 4), PS(b, 0, 416), A_.subtract)
-    mm(0, 128, "pw", 128, "uq", 0)
+    for b in (0, 1):
+        tt(V("left", b, 1536, 4), V("vt", b, 1536, 4), PS(b, 0, 384), A_.subtract)
+    offsets(rk, 0)
     mm(1, 128, "uq", 0, "pw", 128)
+    tt(V("left", 2, 1536, 4), V("vt", 2, 1536, 4), PS(2, 0, 384), A_.subtract)
+    mm(2, 128, "pw", 128, "uq", 0)
+    copy(V("ofd", 8 * rk, 8 * rk + 6), PS(0, 0, 6))
+    copy(V("mn", 0, 6), PS(0, 0, 6))
+    tt(V("left", 3, 1536, 4), V("vt", 3, 1536, 4), PS(3, 0, 384), A_.subtract)
+    dense(rk)
+    quant("qb", 768, 384, "left", 0)
     sel(lo("on", 608, 992), lo("one", 0, 384), [[0, 24], [1, 4], [-1, 4]], A_.is_equal, 0.0, 0, 0)
+    iota(V("f35", 0, 608), [[0, 608]], 0, 0)
     sel(V("thr3a", 0, 96), V("zt", 0, 96), [[-4, 24], [0, 4]], A_.is_ge, -1000.0, 0, 1)
     sel(V("thr6a", 0, 6), V("zt", 0, 6), [[-16, 6]], A_.is_ge, -1000.0, 0, 1)
     sel(V("thr3", 0, 96), V("thr3a", 0, 96), [[4, 24], [0, 4]], A_.is_ge, -1000.0, 3, -1)
     sel(V("thr6", 0, 6), V("thr6a", 0, 6), [[16, 6]], A_.is_ge, -1000.0, 15, -1)
-    for name in ("mh", "ml", "f3", "f5"):
-        iota(V(name, 0, 512), [[0, 512]], 0, 0)
     act(hi("wtl", 128, 160), hi("one", 0, 32), scale=rk / 32.0)
     act(lo("on", 992, 1120), lo("zt", 0, 128))
     for t in (0, 2, 3):
@@ -375,129 +384,117 @@ def rank_program(g, core, T, topo):
     act(hi("on", 993, 1120, 4), hi("zt", 0, 32))
     act(hi("on", 609, 992, 4), hi("one", 0, 96), scale=-1.0)
     SF, UN, NM, BFT = [V("cg", c, c + 1) for c in range(4)]
-    act(SF, PS(0, 0, 1), F_.Identity, scale=2.0 ** 23)
     sizes("zw", 128, 96, 1)
-
-    def place(s):
-        return ("send", 160) if s == rk else ("land%d" % ((s - rk - 1) % N), 0)
-
-    def offsets(s):
-        mm(s, 128, "aoq", 0, place(s)[0], place(s)[1] + 10)
-
-    def dense(s):
-        w, c = place(s)
-        pick("den", 128 * s, w, c, c + 138, "ofd", 8 * s, 8 * s + 8)
+    act(SF, PS(2, 0, 1), F_.Identity, scale=2.0 ** 23)
+    act(V("cf", 6, 7), P8, F_.Copy, scale=4.0)
+    act(V("cf", 7, 8), P7, F_.Copy, scale=4.0)
+    act(hi("a3", 0, 512), hi("zt", 0, 512))
 
     far = [s for s in range(N) if s != rk]
-    offsets(rk)
-    copy(V("ofd", 8 * rk, 8 * rk + 6), PS(rk, 0, 6))
-    copy(V("mn", 0, 6), PS(rk, 0, 6))
-    dense(rk)
-    for s in far:
-        offsets(s)
+    for i, s in enumerate(far):
+        offsets(s, i)
     for s in range(N):
         if s == far[0]:
-            for x in far:
-                copy(V("ofd", 8 * x, 8 * x + 6), PS(x, 0, 6))
-            dense(far[0])
             for i in (0, 1):
-                tt(V("mn", 6 * i + 6, 6 * i + 12), PS(far[i], 0, 6), V("mn", 6 * i, 6 * i + 6), A_.min)
+                copy(V("ofd", 8 * far[i], 8 * far[i] + 6), PS(i, 0, 6))
+            dense(far[0])
+            copy(V("ofd", 8 * far[2], 8 * far[2] + 6), PS(2, 0, 6))
         elif s == far[1]:
             dense(s)
-            tt(V("mn", 18, 24), PS(far[2], 0, 6), V("mn", 12, 18), A_.min)
+            for i in (0, 1):
+                tt(V("mn", 6 * i + 6, 6 * i + 12), PS(i, 0, 6), V("mn", 6 * i, 6 * i + 6), A_.min)
         elif s == far[2]:
             dense(s)
+            tt(V("mn", 18, 24), PS(2, 0, 6), V("mn", 12, 18), A_.min)
         for b in range(4):
-            mm(4 + b, 128, "eq", 128 * b, "den", 128 * s, False, s == N - 1)
+            mm(4 + b, 128, "eq", 128 * b, "den", 96 * (3 - s), False, s == N - 1)
+    quant("onq", 152, 128, "on", 608)
     ts(V("pu", 0, 6), V("mn", 18, 24), 48.0, A_.is_ge, 128.0, A_.mult)
     ts(V("cf", 5, 6), PK, 96.0, A_.mult, V("cf", 4, 5), A_.add)
-    ts(V("cf", 6, 7), P8, 4.0, A_.mult)
     tt(V("pl", 0, 6), V("pu", 0, 6), V("mc", 0, 6), A_.add)
     tt(V("pm", 0, 6), V("pu", 0, 6), V("mask24", 0, 6), A_.mult)
-    ts(V("cf", 7, 8), P7, 4.0, A_.mult)
+    ts(V("ofw", 0, 1), XB8, 288.0, A_.add)
     copy(V("ofp", 0, 6), V("pl", 0, 6))
     run("v", lambda: g.vector.tensor_reduce(ap(UN), ap(V("pm", 0, 6)), AxisListType.X, A_.add), [UN], [V("pm", 0, 6)])
+    for k in range(4):
+        ts(lo("a3", k, 512, 4), lo("s16", 0, 128), V("cf", 8 + k, 9 + k, 1, 0, 96), A_.is_equal, 768.0, A_.mult)
+    ts(NM, UN, 0.0, A_.is_equal, 2.0 ** 30, A_.mult)
+    ts(BFT, UN, SF, A_.mult, 2.0 ** -87, A_.add)
     for b in range(4):
         copy(V("at", b, 384, 4), PS(4 + b, 0, 96))
-        if b == 1:
-            ts(NM, UN, 0.0, A_.is_equal, 2.0 ** 30, A_.mult)
-            ts(BFT, UN, SF, A_.mult, 2.0 ** -87, A_.add)
     quant("pw", 0, 128, "at", 0)
-    pick_codes("pb", 0, "pw", 0, 256, "ofp", 0, 6)
     mm(1, 128, "pw", 0, "uq", 0)
     mm(0, 128, "uq", 0, "pw", 0)
+    pick_codes("pb", 0, "pw", 0, 256, "ofp", 0, 6)
     act(V("sa", 4, 5), PS(1, 0, 1), F_.Abs, bias=BFT, scale=NM)
     sizes("zw", 0, 96, 0)
     pick_scales("pb", 0, "pw", 0, 256, "ofp", 0, 6)
-    act(lo("mh", 0, 16), lo("mk", 0, 16), scale=V("cf", 6, 7, 1, 0, 96))
-    act(lo("ml", 0, 16), lo("mk", 0, 16), scale=V("cf", 7, 8, 1, 0, 96))
-    act(hi("ml", 0, 16), hi("mk", 0, 16))
+    mm(7, 128, "ttq", 0, "onq", 152)
+    act(lo("hm", 0, 16), lo("mk", 0, 16), scale=V("cf", 6, 7, 1, 0, 96))
+    act(lo("hm", 16, 32), lo("mk", 0, 16), scale=V("cf", 7, 8, 1, 0, 96))
+    act(hi("hm", 16, 32), hi("mk", 0, 16))
     zero("left2", 384, 512)
-    for k in range(4):
-        ts(lo("a3", k, 512, 4), lo("s16", 0, 128), V("cf", 8 + k, 9 + k, 1, 0, 96), A_.is_equal, 768.0, A_.mult)
     ts(V("ss2", 0, 96), V("tri", 0, 96), V("sa", 4, 5), A_.mult, V("sa", 4, 5), A_.add)
+    tt(lo("f35", 0, 96), PS(7, 0, 96, 1, 0, 96), lo("thr3", 0, 96), A_.is_lt)
     tt(V("tt", 0, 384, 4), V("zw", 0, 224), V("ss2", 0, 96), A_.is_lt, V("ofp", 0, 6))
-    quant("onq", 152, 128, "on", 608)
+    ts(V("posc", 0, 24), V("pos", 0, 24), V("cf", 5, 6), A_.add, P42, A_.add)
     quant("ttr", 0, 128, "tt", 0)
     mm(2, 128, "ttr", 0, "onq", 0)
     quant("a3q", 0, 128, "a3", 0)
-    quant("mhq", 0, 128, "mh", 0)
+    quant("f3q", 0, 128, "f35", 0)
     for t in range(2):
         ts(lo("wtl", t, 128, 4), PS(2, 0, 32, 1, 0, 96), 0.0, A_.is_equal)
-    ts(V("posc", 0, 24), V("pos", 0, 24), V("cf", 5, 6), A_.add, P42, A_.add)
+    ts(lo("wtl", 128, 160), PS(2, 0, 32, 1, 0, 96), 0.0, A_.is_equal)
     quant("lq", 0, 128, "wtl", 0)
     mm(3, 128, "ahlq", 0, "lq", 0)
-    ts(lo("wtl", 128, 160), PS(2, 0, 32, 1, 0, 96), 0.0, A_.is_equal)
-    quant("mlq", 0, 128, "ml", 0)
     quant("pb", 256, 128, "wtl", 0)
+    mm(1, 128, "a3q", 0, "f3q", 0)
     scan("sc2", 32, 3)
-    for b in range(4):
-        mm(4 + b, 128, "eq", 128 * b, "pb", 0)
-    mm(0, 128, "ttq", 0, "onq", 152)
-    mm(2, 128, "ttr", 0, "onq", 152)
+    mm(0, 128, "ttr", 0, "onq", 152)
+    tt(V("et", 0, 24), PS(1, 0, 24), V("posc", 0, 24), A_.add)
     ts(V("ofw", 1, 3), V("sc2", 15, 32, 16), CORR, A_.subtract)
-    pick("ws", 0, "pb", 0, 384, "ofw", 0, 3)
-    send("ws", [8] * 3, ["wl", "wl", "wl"], [48 + 40 * x for x in range(3)], 40, ["arw0", "arw1", "arw2"])
+    copy(V("ofe", 0, 24), V("et", 0, 24))
+    pick("den", 0, "pb", 0, 384, "ofw", 0, 3)
+    send("den", [8] * 3, ["wl", "wl", "wl"], [40 * x for x in range(3)], 40, ["arw0", "arw1", "arw2"])
     for x in range(3):
-        c0 = 48 + 40 * x
+        c0 = 40 * x
         note(("arw%d" % x, arrive[x], {}), "far", [V("wlc", c0, c0 + 40), V("wls", c0, c0 + 40)], [])
 
-    tt(lo("f3", 0, 96), PS(0, 0, 96, 1, 0, 96), lo("thr3", 0, 96), A_.is_lt)
-    tt(lo("f5", 0, 24, 4), PS(2, 0, 24, 4, 0, 96), lo("thr6", 0, 6), A_.is_lt)
-    pick("wl", 0, "pb", 0, 384, "ofw", 0, 3)
-    quant("f3q", 0, 128, "f3", 0)
-    mm(1, 128, "a3q", 0, "f3q", 0)
-    quant("f5q", 0, 128, "f5", 0)
+    for b in range(4):
+        mm(4 + b, 128, "eq", 128 * b, "pb", 0)
+    tt(lo("f35", 96, 120, 4), PS(0, 0, 24, 4, 0, 96), lo("thr6", 0, 6), A_.is_lt)
+    quant("hmq", 0, 132, "hm", 0)
+    quant("f5q", 0, 128, "f35", 96)
     mm(3, 128, "aoq", 0, "f5q", 0)
-    quant("qb", 768, 416, "left", 0)
-    tt(V("et", 0, 24), PS(1, 0, 24), V("posc", 0, 24), A_.add)
+    for b in range(4):
+        tt(V("left2", b, 384, 4), V("at", b, 384, 4), PS(4 + b, 0, 96), A_.subtract)
     ts(V("et2", 0, 6), PS(3, 0, 6), 128.0, A_.mult)
-    for b in (0, 1):
-        tt(V("left2", b, 384, 4), V("at", b, 384, 4), PS(4 + b, 0, 96), A_.subtract)
-    copy(V("ofe", 0, 24), V("et", 0, 24))
-    tt(V("et2", 6, 12), V("et2", 0, 6), V("mc", 0, 6), A_.add)
-    for b in (2, 3):
-        tt(V("left2", b, 384, 4), V("at", b, 384, 4), PS(4 + b, 0, 96), A_.subtract)
-    pick("oe", 0, "qb", 0, 1184, "ofe", 0, 24)
-    dma("s", None, V("oec", 0, 384), oap=T.oc[:, 0:1536], iap=T.oec[:, 0:384].bitcast(dt.uint8))
     quant("pb", 128, 128, "left2", 0)
-    copy(V("ofo", 0, 6), V("et2", 6, 12))
+    tt(V("et2", 6, 12), V("et2", 0, 6), V("mc", 0, 6), A_.add)
     quant("wq", 0, 128, "wt", 0)
+    copy(V("ofo", 0, 6), V("et2", 6, 12))
+    mm(6, 128, "wq", 0, "den", 8)
+    mm(2, 128, "den", 8, "hmq", 0, True, False)
+    mm(2, 128, "den", 8, "hmq", 4, False, True)
+    pick("oe", 0, "qb", 0, 1152, "ofe", 0, 24)
+    dma("s", None, V("oec", 0, 384), oap=T.oc[:, 0:1536], iap=T.oec[:, 0:384].bitcast(dt.uint8))
     pick("oe", 384, "pb", 0, 256, "ofo", 0, 6)
+    copy(V("nbs", 4, 8), PS(2, 0, 4))
+    act(V("ysb", 32 * rk, 32 * rk + 32), PS(6, 8, 40))
     dma("s", None, V("oec", 384, 480), oap=T.oc[:, 1536:1920], iap=T.oec[:, 384:480].bitcast(dt.uint8))
     for k in range(4):
         dma("s", None, V("oes", 0, 480, 1, 32 * k, 32 * k + 4), oap=T.osc[4 * k:4 * k + 4, :])
+    dma("s", None, V("nbs", 4, 8, 1, 0, 8), oap=T.nb[:, 32 * rk:32 * rk + 32])
 
-    mm(4, 160, "wq", 0, "wl", 8)
-    mm(5, 128, "wl", 8, "mhq", 0, True, False)
-    mm(5, 128, "wl", 8, "mlq", 0, False, True)
-    order = [rk] + own[:3]
-    for b in range(4):
-        act(V("ysb", 32 * order[b], 32 * order[b] + 32), PS(4, 40 * b + 8, 40 * b + 40))
+    mm(4, 128, "wq", 0, "wl", 0)
+    mm(5, 128, "wl", 0, "hmq", 0, True, False)
+    mm(5, 128, "wl", 0, "hmq", 4, False, True)
+    for b in range(3):
+        act(V("ysb", 32 * own[b], 32 * own[b] + 32), PS(4, 40 * b + 8, 40 * b + 40))
     copy(V("nbs", 0, 4), PS(5, 0, 4))
     dma("a", None, V("ysb", 0, 128), oap=T.y[:, :])
-    for b in range(4):
-        o = order[b]
+    for b in range(3):
+        o = own[b]
         dma("s", None, V("nbs", 0, 4, 1, 40 * b, 40 * b + 8), oap=T.nb[:, 32 * o:32 * o + 32])
 
     g.wait_ge(T.sem.ls, left_)

from concourse.bass import DstId, RemoteDMATransfer
from concourse.mybir import dt, AluOpType, ActivationFunctionType, AxisListType

N, P, B, K = 4, 384, 96, 32
F32, BF, I32, U16, CODE, PLANE = "float32", "bfloat16", "int32", "uint16", "float8_e4m3fn_x4", "uint8"
STEP = 1.25 * 2.0 ** -24

SCRATCH = {"ps": ("psum", [128, 4096], F32)}
for _n, _w, _d in (
        ("ert", 1536, BF), ("grt", 1536, BF), ("fot", 512, BF), ("wt", 512, BF), ("uc", 4, BF), ("ucf", 4, F32),
        ("one", 512, BF), ("cst", 96, BF), ("zt", 512, BF), ("ew", 520, BF), ("urep", 512, BF), ("tri", 96, BF), ("s16", 128, BF),
        ("hh", 128, BF), ("mask24", 24, BF), ("mask24a", 24, BF), ("on", 1120, BF), ("tt", 512, BF), ("lt", 608, BF), ("ahl", 512, BF),
        ("ao", 512, BF), ("a3", 512, BF), ("f35", 608, BF), ("wtl", 512, BF), ("mk", 16, BF),
        ("hm", 528, BF), ("vt", 1536, BF), ("left", 1536, BF), ("at", 512, BF), ("left2", 512, BF),
        ("d16", 128, BF), ("sm1", 128, BF), ("sm2", 128, BF), ("sm", 128, BF), ("thr3", 96, BF), ("thr3a", 96, BF), ("thr6", 6, BF), ("thr6a", 6, BF),
        ("icol", 8, I32), ("ci", 8, F32), ("cf", 16, F32), ("cg", 8, F32), ("k6", 4, F32), ("pos", 24, F32), ("posc", 24, F32), ("mcb", 6, F32), ("mc", 6, F32),
        ("sa", 8, F32), ("z", 384, F32), ("ss", 384, F32), ("zw", 224, F32), ("ss2", 96, F32),
        ("sc", 128, F32), ("sc2", 32, F32), ("mn", 24, F32), ("pu", 6, F32), ("pm", 6, F32), ("pl", 6, F32), ("et", 24, F32), ("et2", 12, F32),
        ("ysb", 128, F32), ("nbs", 8, F32),
        ("ofs", 10, U16), ("ofo3", 4, U16), ("ofd", 32, U16), ("ofp", 6, U16), ("ofw", 4, U16), ("ofe", 24, U16), ("ofo", 6, U16)):
    SCRATCH[_n] = ("sbuf", [128, _w], _d)
for _n, _w in (("erq", 384), ("eq", 512), ("uq", 128), ("onq", 280), ("ttq", 128), ("ttr", 128), ("ahlq", 128), ("aoq", 128),
               ("a3q", 128), ("f3q", 128), ("f5q", 128), ("hmq", 132), ("wq", 128), ("lq", 128), ("qb", 1152), ("send", 336),
               ("land0", 176), ("land1", 176), ("land2", 176), ("den", 416), ("pw", 256), ("pb", 384), ("wl", 128), ("oe", 480)):
    SCRATCH[_n + "c"] = ("sbuf", [128, _w], CODE)
    SCRATCH[_n + "s"] = ("sbuf", [128, _w], PLANE)
SEMAPHORES = ["qv", "qa", "qt", "qg", "ls", "arr0", "arr1", "arr2", "arw0", "arw1", "arw2"] + ["d%d" % _i for _i in range(40)]


def rank_program(g, core, T, topo):
    rk = T.rank_of(core)
    if rk is None:
        return
    A_, F_ = AluOpType, ActivationFunctionType
    QUEUE = {"v": g.vector, "a": g.scalar, "t": g.tensor, "g": g, "s": g.sync}
    own = [(rk + 1 + k) % N for k in range(N)]

    known = {q: {} for q in QUEUE}
    count = {"v": 0, "a": 0, "t": 0, "g": 0}
    hist, ndma, dma_tok = {}, [0], []

    def V(name, c0, c1, step=1, p0=0, p1=128):
        return (name, c0, c1, step, p0, p1)

    def PS(bank, c0, c1, step=1, p0=0, p1=128):
        return ("ps", 512 * bank + c0, 512 * bank + c1, step, p0, p1)

    def ap(v):
        return T[v[0]][v[4]:v[5], v[1]:v[2]] if v[3] == 1 else T[v[0]][v[4]:v[5], v[1]:v[2]:v[3]]

    def meet(a, b, one):
        if a[0] == "ps" and not one:
            return a[1] // 512 == b[1] // 512
        if a[1] >= b[2] or b[1] >= a[2] or a[4] >= b[5] or b[4] >= a[5]:
            return False
        return not (a[3] == b[3] and a[3] > 1 and (a[1] - b[1]) % a[3])

    def wait(q, toks):
        for s, v, c in sorted(toks, key=lambda x: -len(x[2])):
            if known[q].get(s, 0) >= v:
                continue
            if any(o[2].get(s, 0) >= v for o in toks if (o[0], o[1]) != (s, v) and known[q].get(o[0], 0) < o[1]):
                continue
            QUEUE[q].wait_ge(T.sem[s], v)
            for k2, v2 in c.items():
                known[q][k2] = max(known[q].get(k2, 0), v2)
            known[q][s] = v

    def need(q, outs, ins, who):
        toks = {}
        for v in ins:
            for (w, tok, by, x) in hist.get(v[0], []):
                if meet(v, x, by == who) and (w or (v[0] == "ps" and by != who)):
                    toks[tok[:2]] = tok
        for v in outs:
            for (w, tok, by, x) in hist.get(v[0], []):
                if meet(v, x, by == who) and not (by == who == "t"):
                    toks[tok[:2]] = tok
        wait(q, list(toks.values()))

    def note(tok, by, outs, ins):
        for w, vs in ((True, outs), (False, ins)):
            for v in vs:
                hist.setdefault(v[0], []).append((w, tok, by, v))

    def run(q, call, outs, ins):
        need(q, outs, ins, q)
        count[q] += 1
        s = "q" + q
        call().then_inc(T.sem[s], 1)
        tok = (s, count[q], dict(known[q]))
        tok[2][s] = count[q]
        note(tok, q, outs, ins)

    def dma(q, out, src, oap=None, iap=None):
        i = ndma[0]
        ndma[0] += 1
        outs, ins = ([out] if out else []), ([src] if src else [])
        need(q, outs, ins, "d%d" % i)
        QUEUE[q].dma_start(oap if oap is not None else ap(out), iap if iap is not None else ap(src)).then_inc(T.sem["d%d" % i], 16)
        tok = ("d%d" % i, 16, dict(known[q]))
        note(tok, "d%d" % i, outs, ins)
        dma_tok.append((q, tok))

    def fill(v, x):
        run("v", lambda: g.vector.memset(ap(v), x), [v], [])

    def copy(o, i):
        run("v", lambda: g.vector.tensor_copy(ap(o), ap(i)), [o], [i])

    def tt(o, a, b, op, off=None):
        if off is None:
            run("v", lambda: g.vector.tensor_tensor(ap(o), ap(a), ap(b), op), [o], [a, b])
        else:
            run("v", lambda: g.vector.tensor_tensor(ap(o), ap(a).indirect(ap(off)), ap(b), op), [o], [a, b, off])

    def ts(o, a, s1, op0, s2=None, op1=None):
        sc = [s for s in (s1, s2) if isinstance(s, tuple)]
        x1 = ap(s1) if isinstance(s1, tuple) else s1
        x2 = ap(s2) if isinstance(s2, tuple) else s2
        if op1 is None:
            run("v", lambda: g.vector.tensor_scalar(ap(o), ap(a), x1, None, op0), [o], [a] + sc)
        else:
            run("v", lambda: g.vector.tensor_scalar(ap(o), ap(a), x1, x2, op0, op1), [o], [a] + sc)

    def act(o, i, func=F_.Copy, bias=0.0, scale=1.0):
        sc = [s for s in (bias, scale) if isinstance(s, tuple)]
        b = ap(bias) if isinstance(bias, tuple) else bias
        s = ap(scale) if isinstance(scale, tuple) else scale
        run("a", lambda: g.scalar.activation(ap(o), ap(i), func, bias=b, scale=s), [o], [i] + sc)

    def zero(name, c0, c1):
        act(V(name, c0, c1), V("zt", 0, c1 - c0))

    def quant(name, c0, n, src, s0):
        o, os, i = V(name + "c", c0, c0 + n), V(name + "s", c0, c0 + n), V(src, s0, s0 + 4 * n)
        run("v", lambda: g.vector.quantize_mx(ap(o), ap(os), ap(i)), [o, os], [i])

    def mm(bank, n, l, l0, r, r0, start=True, stop=True):
        o = PS(bank, 0, n)
        a, b = V(l + "c", l0, l0 + 128), V(l + "s", l0, l0 + 128)
        c, d = V(r + "c", r0, r0 + n), V(r + "s", r0, r0 + n)
        run("t", lambda: g.tensor.matmul_mx(ap(o), ap(a), ap(b), ap(c), ap(d), start, stop), [o], [a, b, c, d])

    def pick_codes(o, o0, w, w0, w1, off, k0, k1):
        n, f = 16 * (k1 - k0), V(off, k0, k1)
        a, b = V(o + "c", o0, o0 + n), V(w + "c", w0, w1)
        run("v", lambda: g.vector.tensor_copy(ap(a).bitcast(dt.uint32), ap(b).bitcast(dt.uint32).indirect(ap(f))), [a], [b, f])

    def pick_scales(o, o0, w, w0, w1, off, k0, k1):
        n, f = 16 * (k1 - k0), V(off, k0, k1)
        c, d = V(o + "s", o0, o0 + n), V(w + "s", w0, w1)
        run("a", lambda: g.scalar.activation(ap(c), ap(d).indirect(ap(f)), F_.Copy), [c], [d, f])

    def pick(*a):
        pick_codes(*a)
        pick_scales(*a)

    def scan(o, n, bank):
        run("v", lambda: g.vector.tensor_tensor_scan(ap(V(o, 0, n)), ap(V("sm", 0, n)), ap(PS(bank, 0, n)), 0.0, A_.add, A_.max),
            [V(o, 0, n)], [V("sm", 0, n), PS(bank, 0, n)])

    def sel(o, i, pattern, op, fillv, base, cm):
        run("g", lambda: g.affine_select(ap(o), ap(i), pattern, op, fillv, base, cm), [o], [i])

    def iota(o, pattern, base, cm, small=True):
        if small:
            run("g", lambda: g.iota(ap(o), pattern, base, cm, allow_small_or_imprecise_dtypes=True), [o], [])
        else:
            run("g", lambda: g.iota(ap(o), pattern, base, cm), [o], [])

    def lo(name, c0, c1, step=1):
        return V(name, c0, c1, step, 0, 96)

    def hi(name, c0, c1, step=1):
        return V(name, c0, c1, step, 96, 128)

    dma("s", V("ert", 0, 768), None, iap=T.er[:, 0:768])
    dma("a", V("uc", 0, 4), None, iap=T.u[:, 0:4])
    dma("a", V("ert", 768, 1536), None, iap=T.er[:, 768:1536])
    dma("s", V("grt", 0, 1536), None, iap=T.gr[:, :])
    wait("s", [dma_tok[2][1]])
    dma("s", V("fot", 0, 384), None, iap=T.fo[:, :])
    dma("s", V("wt", 0, 512), None, iap=T.w[:, :])

    iota(V("icol", 0, 1), [[0, 1]], 0, 1, small=False)
    iota(V("icol", 5, 6), [[0, 1]], N - 1 - rk, 1, small=False)
    fill(V("one", 0, 128), 1.0)
    fill(V("ew", 0, 520), 0.0)
    sel(V("ew", 3, 515, 4), V("one", 0, 128), [[-1, 128]], A_.is_equal, 0.0, 0, 1)
    iota(V("s16", 0, 128), [[0, 8], [1, 16]], 0, 0)
    fill(V("zt", 0, 512), 0.0)
    act(V("one", 128, 512), V("zt", 0, 384), F_.Identity, bias=1.0)
    for c, x in ((1, 15), (2, 7), (3, 3)):
        ts(V("icol", c, c + 1), V("icol", 0, 1), x, A_.bitwise_and)
    ts(V("icol", 4, 5), V("icol", 0, 1), 15, A_.bitwise_and, 2, A_.logical_shift_right)
    ts(V("icol", 6, 7), V("icol", 5, 6), 3, A_.bitwise_and)
    fill(V("cst", 0, 96), STEP)
    P0, P15, P7, P3, P42, PK = [V("ci", c, c + 1) for c in (0, 1, 2, 3, 4, 6)]
    P8, CORR, XB8, TINY = [V("cf", c, c + 1) for c in (0, 1, 3, 15)]
    copy(V("ci", 0, 7), V("icol", 0, 7))
    iota(V("hh", 0, 128), [[0, 4], [1, 2], [0, 16]], 0, 0)
    iota(V("k6", 0, 4), [[6, 4]], 734, 0)
    sel(V("tri", 0, 96), V("cst", 0, 96), [[1, 96]], A_.is_gt, 0.0, 0, -1)
    for b in range(4):
        quant("eq", 128 * b, 128, "ew", 3 - b)
        if b == 0:
            tt(P8, P0, P7, A_.subtract)
            fill(TINY, 2.0 ** -87)
    quant("erq", 0, 192, "ert", 0)
    quant("erq", 192, 192, "ert", 768)
    quant("qb", 384, 128, "zt", 0)
    for name, c, n in (("land0", 48, 90), ("land1", 48, 90), ("land2", 48, 90), ("send", 208, 90), ("pb", 96, 32), ("den", 384, 32), ("wl", 120, 8)):
        o, i = V(name + "c", c, c + n), V("qbc", 384, 384 + n)
        dma("s", o, i, ap(o).bitcast(dt.uint8), ap(i).bitcast(dt.uint8))
        dma("s", V(name + "s", c, c + n), V("qbs", 384, 384 + n))
    sel(lo("on", 0, 512), lo("one", 0, 512), [[1, 4], [0, 32], [-1, 4]], A_.is_equal, 0.0, 0, 0)
    sel(lo("on", 512, 608), lo("one", 0, 96), [[1, 4], [0, 6], [-1, 4]], A_.is_equal, 0.0, 0, 0)
    iota(V("pos", 0, 24), [[4, 24]], 192, 0)
    iota(V("mcb", 0, 6), [[16, 6]], 0, 0)

    act(hi("on", 1, 512, 4), hi("s16", 0, 128), scale=-1.0 / 32)
    act(V("ucf", 0, 4), V("uc", 0, 4))
    for t in range(4):
        act(V("urep", t, 512, 4), V("one", 0, 128), scale=V("ucf", t, t + 1))
    act(hi("on", 2, 512, 4), hi("hh", 0, 128), scale=-0.5)
    act(hi("on", 513, 608, 4), hi("zt", 0, 24))
    act(hi("on", 514, 608, 4), hi("one", 0, 24), scale=-0.5)
    for t in (0, 3):
        act(hi("on", t, 608, 4), hi("zt", 0, 152))
    zero("ahl", 0, 512)
    act(lo("ahl", 0, 512, 4), lo("one", 0, 128), scale=P8[:4] + (0, 96))
    act(lo("ahl", 1, 512, 4), lo("one", 0, 128), scale=P7[:4] + (0, 96))
    act(hi("ahl", 1, 512, 4), hi("one", 0, 128))
    act(lo("tt", 384, 512), lo("zt", 0, 128))
    zero("lt", 0, 512)
    zero("lt", 512, 608)

    for b in range(4):
        mm(b, 384, "eq", 128 * b, "erq", 0)
    quant("uq", 0, 128, "urep", 0)
    fill(hi("tt", 0, 512), 1.0)
    at0 = [192, 288, 0, 96]
    for b in range(4):
        for k in range(4):
            tt(V("vt", 4 * at0[k] + b, 4 * at0[k] + 384, 4), PS(b, own[k], 384, 4), V("grt", 4 * own[k] + b, 1536, 16), A_.add)
    quant("qb", 192, 192, "vt", 768)
    quant("qb", 0, 192, "vt", 0)
    iota(V("lt", 1, 512, 4), [[-6, 2], [3, 2], [0, 32]], 6, 0)
    iota(V("lt", 513, 608, 4), [[0, 24]], 1, 0)
    sel(V("mask24a", 0, 24), V("one", 0, 24), [[0, 4], [-16, 6]], A_.is_ge, 0.0, 0, 1)
    sel(V("mask24", 0, 24), V("mask24a", 0, 24), [[0, 4], [16, 6]], A_.is_ge, 0.0, 15, -1)
    sel(V("mk", 0, 16), V("one", 0, 16), [[1, 4], [-1, 4]], A_.is_equal, 0.0, 0, 0)
    iota(V("wtl", 0, 512), [[0, 512]], 0, 0)
    iota(V("hm", 0, 528), [[0, 528]], 0, 0)

    def score(c, bank):
        act(lo("sa", c, c + 1), PS(bank, 0, 1, 1, 0, 96), F_.Abs, bias=TINY[:4] + (0, 96), scale=2.0 ** 30)

    def sizes(o, c0, n, bank, b0=0):
        act(V(o, c0, c0 + n), PS(bank, b0, b0 + n), F_.Abs, bias=TINY, scale=2.0 ** 30)

    def raised(o, c0, c):
        ts(lo(o, c0, c0 + 96), lo("tri", 0, 96), lo("sa", c, c + 1), A_.mult, lo("sa", c, c + 1), A_.add)

    RB, SB = (4, 7), (5, 6, 2, 3)
    for h in range(2):
        mm(SB[2 * h], 128, "qb", at0[2 * h], "uq", 0)
        mm(SB[2 * h + 1], 128, "qb", at0[2 * h + 1], "uq", 0)
        mm(RB[h], 192, "uq", 0, "qb", at0[2 * h])
    quant("onq", 0, 152, "on", 0)
    quant("ahlq", 0, 128, "ahl", 0)
    for h in range(2):
        for k in (2 * h, 2 * h + 1):
            score(k, SB[k])
        for k in (0, 1):
            sizes("z", 192 * h + 96 * k, 96, RB[h], 96 * k)
    for h in range(2):
        for k in (2 * h, 2 * h + 1):
            raised("ss", 96 * k, k)
        if h == 0:
            ts(V("d16", 0, 128), V("s16", 0, 128), P15, A_.subtract)
        for k in (2 * h, 2 * h + 1):
            tt(lo("tt", k, 384, 4), lo("z", 96 * k, 96 * k + 96), lo("ss", 96 * k, 96 * k + 96), A_.is_lt)
    ts(CORR, P15, 15.0, A_.is_lt, 512.0, A_.mult)
    quant("ttq", 0, 128, "tt", 0)
    mm(0, 152, "ttq", 0, "onq", 0)
    ts(V("ofs", 0, 9, 3), V("k6", 0, 3), P15, A_.add)
    ts(V("sm1", 0, 128), V("d16", 0, 128), 0.0, A_.is_equal, -4096.0, A_.mult)
    ts(V("sm2", 0, 128), V("d16", 0, 128), 1.0, A_.is_equal, 512.0, A_.mult)
    act(XB8, P15, F_.Relu, bias=-8.0)
    for k in range(4):
        act(V("cf", 8 + k, 9 + k), P3, F_.Identity, bias=float(own[k]), scale=4.0)
    act(V("mc", 0, 6), V("mcb", 0, 6), F_.Identity, bias=P15)
    zero("ao", 0, 512)
    act(hi("ao", 1, 512, 4), hi("one", 0, 128))
    zero("at", 384, 512)
    zero("zw", 96, 128)
    zero("fot", 384, 512)
    for t in range(2):
        ts(lo("lt", t, 512, 4), PS(0, 0, 128, 1, 0, 96), 0.0, A_.is_equal)
    ts(V("ofo3", 0, 1), V("k6", 3, 4), P15, A_.add)
    quant("qb", 512, 128, "lt", 0)
    mm(1, 128, "ahlq", 0, "qb", 512)
    tt(lo("lt", 512, 608, 4), PS(0, 128, 152, 1, 0, 96), lo("mask24", 0, 24), A_.mult)
    tt(V("sm", 0, 128), V("sm1", 0, 128), V("sm2", 0, 128), A_.add)
    quant("qb", 640, 128, "lt", 96)
    scan("sc", 128, 1)
    ts(V("cf", 4, 5), PK, 2.0, A_.is_ge, -384.0, A_.mult)
    ts(V("ofs", 1, 9, 3), V("sc", 15, 96, 32), CORR, A_.subtract)
    ts(V("ofs", 2, 9, 3), V("sc", 31, 96, 32), CORR, A_.subtract)
    pick("send", 16, "qb", 0, 768, "ofs", 0, 9)
    ts(V("ofo3", 1, 3), V("sc", 111, 128, 16), CORR, A_.subtract)

    eng = topo.engines(core, T.cores[own[0]])
    for k in range(3):
        eng = [e for e in eng if e in topo.engines(core, T.cores[own[k]])]
    q4 = len(eng) // 4
    share = ([eng[0:2 * q4], eng[2 * q4:3 * q4], eng[3 * q4:4 * q4]],
             [eng[2 * q4:4 * q4], eng[0:q4], eng[q4:2 * q4]])

    def send(src, cols, dst, dcol, width, sem):
        for part in (0, 1):
            views, trs = [], []
            for k in range(3):
                m = 0
                for e in share[part][k]:
                    m |= 1 << e
                rid, pid = topo.addr(T.cores[own[k]])[0:2]
                sv = V(src + "cs"[part], cols[k], cols[k] + width)
                dv = V(dst[2 - k] + "cs"[part], dcol[2 - k], dcol[2 - k] + width)
                s_, d_ = (ap(sv).bitcast(dt.uint8), ap(dv).bitcast(dt.uint8)) if part == 0 else (ap(sv), ap(dv))
                views.append(sv)
                trs.append(RemoteDMATransfer(dst_ids=[DstId(rid=rid, pnc=pid)], dma_engine_mask=m, remote_sem=T.sem[sem[2 - k]], src=s_, dst=d_))
            need("g", [], views, "g")
            g.remote_dma_fused(trs, local_sem=T.sem.ls)

    arrive = [len(share[0][2 - x]) + len(share[1][2 - x]) for x in range(3)]
    left_ = 2 * sum(arrive)
    send("send", [26 + 48 * k for k in range(3)], ["land0", "land1", "land2"], [10] * 3, 38, ["arr0", "arr1", "arr2"])
    for x in range(3):
        note(("arr%d" % x, arrive[x], {}), "far", [V("land%dc" % x, 10, 48), V("land%ds" % x, 10, 48)], [])

    quant("pw", 128, 128, "fot", 0)
    ts(lo("ao", 0, 512, 4), lo("s16", 0, 128), P15[:4] + (0, 96), A_.is_equal)
    pick("send", 160, "qb", 0, 768, "ofo3", 0, 3)
    quant("aoq", 0, 128, "ao", 0)

    def place(s):
        return ("send", 160) if s == rk else ("land%d" % ((s - rk - 1) % N), 0)

    def offsets(s, bank):
        mm(bank, 128, "aoq", 0, place(s)[0], place(s)[1] + 10)

    def dense(s):
        w, c = place(s)
        pick("den", 96 * (3 - s), w, c, c + 138, "ofd", 8 * s, 8 * s + 6)

    for b in range(4):
        mm(b, 384, "eq", 128 * b, "qb", 0)
    for b in range(4):
        mm(4 + b, 128, "eq", 128 * b, "pw", 128, True, False)
    for b in (0, 1):
        tt(V("left", b, 1536, 4), V("vt", b, 1536, 4), PS(b, 0, 384), A_.subtract)
    offsets(rk, 0)
    mm(1, 128, "uq", 0, "pw", 128)
    tt(V("left", 2, 1536, 4), V("vt", 2, 1536, 4), PS(2, 0, 384), A_.subtract)
    mm(2, 128, "pw", 128, "uq", 0)
    copy(V("ofd", 8 * rk, 8 * rk + 6), PS(0, 0, 6))
    copy(V("mn", 0, 6), PS(0, 0, 6))
    tt(V("left", 3, 1536, 4), V("vt", 3, 1536, 4), PS(3, 0, 384), A_.subtract)
    dense(rk)
    quant("qb", 768, 384, "left", 0)
    sel(lo("on", 608, 992), lo("one", 0, 384), [[0, 24], [1, 4], [-1, 4]], A_.is_equal, 0.0, 0, 0)
    iota(V("f35", 0, 608), [[0, 608]], 0, 0)
    sel(V("thr3a", 0, 96), V("zt", 0, 96), [[-4, 24], [0, 4]], A_.is_ge, -1000.0, 0, 1)
    sel(V("thr6a", 0, 6), V("zt", 0, 6), [[-16, 6]], A_.is_ge, -1000.0, 0, 1)
    sel(V("thr3", 0, 96), V("thr3a", 0, 96), [[4, 24], [0, 4]], A_.is_ge, -1000.0, 3, -1)
    sel(V("thr6", 0, 6), V("thr6a", 0, 6), [[16, 6]], A_.is_ge, -1000.0, 15, -1)
    act(hi("wtl", 128, 160), hi("one", 0, 32), scale=rk / 32.0)
    act(lo("on", 992, 1120), lo("zt", 0, 128))
    for t in (0, 2, 3):
        act(hi("on", 608 + t, 1120, 4), hi("zt", 0, 128))
    act(hi("on", 993, 1120, 4), hi("zt", 0, 32))
    act(hi("on", 609, 992, 4), hi("one", 0, 96), scale=-1.0)
    SF, UN, NM, BFT = [V("cg", c, c + 1) for c in range(4)]
    sizes("zw", 128, 96, 1)
    act(SF, PS(2, 0, 1), F_.Identity, scale=2.0 ** 23)
    act(V("cf", 6, 7), P8, F_.Copy, scale=4.0)
    act(V("cf", 7, 8), P7, F_.Copy, scale=4.0)
    act(hi("a3", 0, 512), hi("zt", 0, 512))

    far = [s for s in range(N) if s != rk]
    for i, s in enumerate(far):
        offsets(s, i)
    for s in range(N):
        if s == far[0]:
            for i in (0, 1):
                copy(V("ofd", 8 * far[i], 8 * far[i] + 6), PS(i, 0, 6))
            dense(far[0])
            copy(V("ofd", 8 * far[2], 8 * far[2] + 6), PS(2, 0, 6))
        elif s == far[1]:
            dense(s)
            for i in (0, 1):
                tt(V("mn", 6 * i + 6, 6 * i + 12), PS(i, 0, 6), V("mn", 6 * i, 6 * i + 6), A_.min)
        elif s == far[2]:
            dense(s)
            tt(V("mn", 18, 24), PS(2, 0, 6), V("mn", 12, 18), A_.min)
        for b in range(4):
            mm(4 + b, 128, "eq", 128 * b, "den", 96 * (3 - s), False, s == N - 1)
    quant("onq", 152, 128, "on", 608)
    ts(V("pu", 0, 6), V("mn", 18, 24), 48.0, A_.is_ge, 128.0, A_.mult)
    ts(V("cf", 5, 6), PK, 96.0, A_.mult, V("cf", 4, 5), A_.add)
    tt(V("pl", 0, 6), V("pu", 0, 6), V("mc", 0, 6), A_.add)
    tt(V("pm", 0, 6), V("pu", 0, 6), V("mask24", 0, 6), A_.mult)
    ts(V("ofw", 0, 1), XB8, 288.0, A_.add)
    copy(V("ofp", 0, 6), V("pl", 0, 6))
    run("v", lambda: g.vector.tensor_reduce(ap(UN), ap(V("pm", 0, 6)), AxisListType.X, A_.add), [UN], [V("pm", 0, 6)])
    for k in range(4):
        ts(lo("a3", k, 512, 4), lo("s16", 0, 128), V("cf", 8 + k, 9 + k, 1, 0, 96), A_.is_equal, 768.0, A_.mult)
    ts(NM, UN, 0.0, A_.is_equal, 2.0 ** 30, A_.mult)
    ts(BFT, UN, SF, A_.mult, 2.0 ** -87, A_.add)
    for b in range(4):
        copy(V("at", b, 384, 4), PS(4 + b, 0, 96))
    quant("pw", 0, 128, "at", 0)
    mm(1, 128, "pw", 0, "uq", 0)
    mm(0, 128, "uq", 0, "pw", 0)
    pick_codes("pb", 0, "pw", 0, 256, "ofp", 0, 6)
    act(V("sa", 4, 5), PS(1, 0, 1), F_.Abs, bias=BFT, scale=NM)
    sizes("zw", 0, 96, 0)
    pick_scales("pb", 0, "pw", 0, 256, "ofp", 0, 6)
    mm(7, 128, "ttq", 0, "onq", 152)
    act(lo("hm", 0, 16), lo("mk", 0, 16), scale=V("cf", 6, 7, 1, 0, 96))
    act(lo("hm", 16, 32), lo("mk", 0, 16), scale=V("cf", 7, 8, 1, 0, 96))
    act(hi("hm", 16, 32), hi("mk", 0, 16))
    zero("left2", 384, 512)
    ts(V("ss2", 0, 96), V("tri", 0, 96), V("sa", 4, 5), A_.mult, V("sa", 4, 5), A_.add)
    tt(lo("f35", 0, 96), PS(7, 0, 96, 1, 0, 96), lo("thr3", 0, 96), A_.is_lt)
    tt(V("tt", 0, 384, 4), V("zw", 0, 224), V("ss2", 0, 96), A_.is_lt, V("ofp", 0, 6))
    ts(V("posc", 0, 24), V("pos", 0, 24), V("cf", 5, 6), A_.add, P42, A_.add)
    quant("ttr", 0, 128, "tt", 0)
    mm(2, 128, "ttr", 0, "onq", 0)
    quant("a3q", 0, 128, "a3", 0)
    quant("f3q", 0, 128, "f35", 0)
    for t in range(2):
        ts(lo("wtl", t, 128, 4), PS(2, 0, 32, 1, 0, 96), 0.0, A_.is_equal)
    ts(lo("wtl", 128, 160), PS(2, 0, 32, 1, 0, 96), 0.0, A_.is_equal)
    quant("lq", 0, 128, "wtl", 0)
    mm(3, 128, "ahlq", 0, "lq", 0)
    quant("pb", 256, 128, "wtl", 0)
    mm(1, 128, "a3q", 0, "f3q", 0)
    scan("sc2", 32, 3)
    mm(0, 128, "ttr", 0, "onq", 152)
    tt(V("et", 0, 24), PS(1, 0, 24), V("posc", 0, 24), A_.add)
    ts(V("ofw", 1, 3), V("sc2", 15, 32, 16), CORR, A_.subtract)
    copy(V("ofe", 0, 24), V("et", 0, 24))
    pick("den", 0, "pb", 0, 384, "ofw", 0, 3)
    send("den", [8] * 3, ["wl", "wl", "wl"], [40 * x for x in range(3)], 40, ["arw0", "arw1", "arw2"])
    for x in range(3):
        c0 = 40 * x
        note(("arw%d" % x, arrive[x], {}), "far", [V("wlc", c0, c0 + 40), V("wls", c0, c0 + 40)], [])

    for b in range(4):
        mm(4 + b, 128, "eq", 128 * b, "pb", 0)
    tt(lo("f35", 96, 120, 4), PS(0, 0, 24, 4, 0, 96), lo("thr6", 0, 6), A_.is_lt)
    quant("hmq", 0, 132, "hm", 0)
    quant("f5q", 0, 128, "f35", 96)
    mm(3, 128, "aoq", 0, "f5q", 0)
    for b in range(4):
        tt(V("left2", b, 384, 4), V("at", b, 384, 4), PS(4 + b, 0, 96), A_.subtract)
    ts(V("et2", 0, 6), PS(3, 0, 6), 128.0, A_.mult)
    quant("pb", 128, 128, "left2", 0)
    tt(V("et2", 6, 12), V("et2", 0, 6), V("mc", 0, 6), A_.add)
    quant("wq", 0, 128, "wt", 0)
    copy(V("ofo", 0, 6), V("et2", 6, 12))
    mm(6, 128, "wq", 0, "den", 8)
    mm(2, 128, "den", 8, "hmq", 0, True, False)
    mm(2, 128, "den", 8, "hmq", 4, False, True)
    pick("oe", 0, "qb", 0, 1152, "ofe", 0, 24)
    dma("s", None, V("oec", 0, 384), oap=T.oc[:, 0:1536], iap=T.oec[:, 0:384].bitcast(dt.uint8))
    pick("oe", 384, "pb", 0, 256, "ofo", 0, 6)
    copy(V("nbs", 4, 8), PS(2, 0, 4))
    act(V("ysb", 32 * rk, 32 * rk + 32), PS(6, 8, 40))
    dma("s", None, V("oec", 384, 480), oap=T.oc[:, 1536:1920], iap=T.oec[:, 384:480].bitcast(dt.uint8))
    for k in range(4):
        dma("s", None, V("oes", 0, 480, 1, 32 * k, 32 * k + 4), oap=T.osc[4 * k:4 * k + 4, :])
    dma("s", None, V("nbs", 4, 8, 1, 0, 8), oap=T.nb[:, 32 * rk:32 * rk + 32])

    mm(4, 128, "wq", 0, "wl", 0)
    mm(5, 128, "wl", 0, "hmq", 0, True, False)
    mm(5, 128, "wl", 0, "hmq", 4, False, True)
    for b in range(3):
        act(V("ysb", 32 * own[b], 32 * own[b] + 32), PS(4, 40 * b + 8, 40 * b + 40))
    copy(V("nbs", 0, 4), PS(5, 0, 4))
    dma("a", None, V("ysb", 0, 128), oap=T.y[:, :])
    for b in range(3):
        o = own[b]
        dma("s", None, V("nbs", 0, 4, 1, 40 * b, 40 * b + 8), oap=T.nb[:, 32 * o:32 * o + 32])

    g.wait_ge(T.sem.ls, left_)
    for q, tok in dma_tok:
        wait(q, [tok])
    for q in ("v", "a", "t", "g"):
        if known["s"].get("q" + q, 0) < count[q]:
            g.sync.wait_ge(T.sem["q" + q], count[q])
